import numpy as np
import ml_dtypes


def mxq(x, axis, fmt="e4m3"):
    dtype, down = {"e4m3": (ml_dtypes.float8_e4m3fn, 7), "e5m2": (ml_dtypes.float8_e5m2, 14)}[fmt]
    v = np.moveaxis(np.asarray(x, np.float32).astype(ml_dtypes.bfloat16).astype(np.float64), axis, -1)
    blocks = v.reshape(v.shape[:-1] + (-1, 32))
    amax = np.abs(blocks).max(-1, keepdims=True)
    byte = np.maximum(np.where(amax > 0, np.frexp(amax)[1] - 1 + 127, 0) - down, 1)
    scale = np.exp2(byte - 127.0)
    codes = (blocks / scale).astype(np.float32).astype(dtype).astype(np.float64)
    return np.moveaxis((codes * scale).reshape(v.shape), -1, axis)


WIDE = False


def mx_kscale(k):
    if not WIDE:
        return np.ones(k)
    levels = np.array([10, -10, 5, -5, 0])
    if k % 512:
        return np.exp2(np.random.permutation(np.resize(levels, k // 32))).repeat(32)
    a = np.empty((k // 512, 16))
    for p in range(k // 512):
        a[p, :8] = np.random.permutation(np.resize(levels, 8))
        for g in range(8):
            far = levels[np.abs(levels - a[p, g]) >= 10]
            a[p, g + 8] = far[np.random.randint(len(far))]
    return np.exp2(a.ravel()).repeat(32)


BF16 = ml_dtypes.bfloat16


def bf(x):
    return np.asarray(x, np.float32).astype(BF16)


def f64(x):
    return np.asarray(x).astype(np.float64)


N, D, V = 1024, 1024, 2048


def log_normalize(logits):
    m = logits.max(axis=-1, keepdims=True)
    return logits - (m + np.log(np.sum(np.exp(logits - m), axis=-1, keepdims=True)))


def jsd_base2(zc, zu):
    lp = log_normalize(zc)
    lq = log_normalize(zu)
    p = np.exp(lp)
    q = np.exp(lq)
    lm = np.log((p + q) / 2.0)
    kl_p = np.sum(p * (lp - lm), axis=-1)
    kl_q = np.sum(q * (lq - lm), axis=-1)
    return (0.5 * kl_p + 0.5 * kl_q) / np.log(2.0)


def draw0():
    s = mx_kscale(D)
    gc = np.random.uniform(0.5, 1.5, (N, 1))
    gu = np.random.uniform(0.5, 1.5, (N, 1))
    return {"hc": bf(np.random.standard_normal((N, D)) * gc * s), "hu": bf(np.random.standard_normal((N, D)) * gu * s),
            "w": bf(np.random.standard_normal((D, V)) * 1.5 / np.sqrt(D) / s[:, None])}


def core(hc, hu, w):
    wq = mxq(f64(w), 0, "e4m3")
    zc = mxq(f64(hc), 1, "e4m3") @ wq
    zu = mxq(f64(hu), 1, "e4m3") @ wq
    a = jsd_base2(zc, zu)[:, None]
    return (1.0 + a) * zc - a * zu


def e4m3fn_bytes(y):
    return np.clip(np.asarray(y, np.float64), -448.0, 448.0).astype(np.float32).astype(ml_dtypes.float8_e4m3fn).view(np.uint8)


def e4m3fn_values(b):
    return np.asarray(b, np.uint8).view(ml_dtypes.float8_e4m3fn).astype(np.float64)


def setup_inputs():
    d = draw0()
    x0 = np.asarray(d['w']).astype(np.float64)
    s = (np.max(np.abs(x0), axis=(1,), keepdims=True) / 448.0).astype(np.float32)
    out = {}
    for k, v in d.items():
        if k == 'w':
            out['w_bytes'] = e4m3fn_bytes(x0 / s.astype(np.float64))
            out['w_scale'] = s
        else:
            out[k] = v
    return out


def reference(hc, hu, w_bytes, w_scale):
    return core(hc, hu, e4m3fn_values(w_bytes) * w_scale.astype(np.float64))

@@ -1,0 +1,433 @@
+import math
+from contextlib import ExitStack
+
+import concourse.mybir as mybir
+from concourse.masks import make_identity
+
+N, D, V = 1024, 1024, 2048
+FLOPS = 2 * 2 * N * D * V
+
+F32 = mybir.dt.float32
+BF16 = mybir.dt.bfloat16
+U32 = mybir.dt.uint32
+U8 = mybir.dt.uint8
+FP8 = mybir.dt.float8_e4m3fn
+FP8X4 = mybir.dt.float8_e4m3fn_x4
+ALU = mybir.AluOpType
+ACT = mybir.ActivationFunctionType
+
+P = 128
+PACK = 4
+PASSES = D // (P * PACK)
+BANK = 512
+CHUNKS = V // BANK
+TILES = N // P
+SLOTS = 4
+D_SLOTS = 3
+Z_BANKS = 6
+LN2 = math.log(2.0)
+SHRINK = 1.0 - 2.0**-24
+STEPS = 256
+LOG_SPAN = math.log(V)
+STEP = 2.0 * LOG_SPAN / STEPS
+
+
+def tile_adacadjsdcontrastlogits_kernel(tc, hc, hu, w_bytes, w_scale, out):
+    nc = tc.nc
+    with ExitStack() as ctx:
+        keep = ctx.enter_context(tc.tile_pool(name="keep", bufs=1))
+        rows = ctx.enter_context(tc.tile_pool(name="rows", bufs=1))
+        stage = ctx.enter_context(tc.tile_pool(name="stage", bufs=2))
+        psum = ctx.enter_context(tc.psum_pool(name="psum", bufs=1))
+        ctx.enter_context(tc.manual_schedule())
+
+        w_view = w_bytes.rearrange("(g p t) n -> g p t n", p=P, t=PACK)
+        pieces = [(n, g) for n in range(CHUNKS) for g in range(PASSES)]
+        w_raw, w_planes, w_grouped, w_codes, w_blocks = {}, {}, {}, {}, {}
+        h_raw, h_turned, h_grouped, h_codes, h_blocks = {}, {}, {}, {}, {}
+        banks, t = {}, {}
+        counts = {"multiplied": 0, "drained": 0}
+
+        def row_tile(role, i, name):
+            return rows.tile([P, V], F32, name="%s%d" % (name, i), tag="%s%d" % (role, i % SLOTS), align_bytes=64)
+
+        def stat(name, i, width):
+            t[name, i] = keep.tile([P, width], F32, name="%s%d" % (name, i))
+            return t[name, i]
+
+        scale = keep.tile([P, PASSES, PACK], F32, name="scale")
+        identity = keep.tile([P, P], F32, name="identity")
+
+        ladder = keep.tile([P, STEPS], F32, name="ladder")
+
+        def load_w(j):
+            n, g = pieces[j]
+            w_raw[j] = stage.tile([P, PACK, BANK], U8, name="w_raw%d" % j, tag="w_raw", bufs=4)
+            nc.sync.dma_start(out=w_raw[j][:], in_=w_view[g][:, :, n * BANK : (n + 1) * BANK])
+
+        def load_h(i):
+            for a, h in enumerate((hc, hu)):
+                h_raw[i, a] = stage.tile([P, D], BF16, name="h_raw%d_%d" % (i, a), tag="h_raw%d" % a)
+                nc.sync.dma_start(out=h_raw[i, a][:], in_=h[i * P : (i + 1) * P, :])
+
+        def widen(j, on_vector=0):
+            g = pieces[j][1]
+            w_planes[j] = rows.tile([P, PACK, BANK], BF16, name="w_planes%d" % j, tag=("ec3", "eu3", "zc3")[j % 3], align_bytes=64)
+            for k in range(PACK):
+                if k < on_vector:
+                    nc.vector.tensor_scalar(out=w_planes[j][:, k, :], in0=w_raw[j][:, k, :].bitcast(FP8), scalar1=scale[:, g, k : k + 1], scalar2=None, op0=ALU.mult)
+                else:
+                    nc.scalar.activation(out=w_planes[j][:, k, :], in_=w_raw[j][:, k, :].bitcast(FP8), func=ACT.Copy, scale=scale[:, g, k : k + 1])
+            if j + 4 < len(pieces):
+                load_w(j + 4)
+
+        def interleave(j, copy):
+            w_grouped[j] = rows.tile([P, BANK, PACK], BF16, name="w_grouped%d" % j, tag=("ec2", "eu2")[j % 2], align_bytes=64)
+            copy(
+                out=w_grouped[j][:].rearrange("p (c i) t -> p c t i", i=4),
+                in_=w_planes[j][:].rearrange("p t (c i) -> p c t i", i=4),
+            )
+
+        def quantize_w(j):
+            w_codes[pieces[j]] = keep.tile([P, BANK], U32, name="w_codes%d" % j, align_bytes=64)
+            w_blocks[pieces[j]] = keep.tile([P, BANK], U8, name="w_blocks%d" % j, align_bytes=64)
+            nc.vector.quantize_mx(
+                out=w_codes[pieces[j]][:].bitcast(FP8X4),
+                scales=w_blocks[pieces[j]][:],
+                in_=w_grouped[j][:].rearrange("p n t -> p (n t)"),
+            )
+            multiply_ahead()
+
+        def turn(i):
+            for a in range(2):
+                words = h_raw[i, a][:].bitcast(F32)
+                h_turned[a] = psum.tile([P, PASSES, 2, P], F32, name="h_turned%d_%d" % (i, a), tag="h_turned%d" % a)
+                for g in range(PASSES):
+                    for u in range(2):
+                        nc.tensor.transpose(h_turned[a][:, g, u, :], words[:, 256 * g + u : 256 * (g + 1) : 2], identity[:])
+            if i + 2 < TILES:
+                load_h(i + 2)
+
+        def regroup(i):
+            if 2 <= i < 2 + D_SLOTS:
+                h_grouped[i] = rows.tile([P, 2, PASSES, P, 2], F32, name="h_grouped%d" % i, tag="d%d" % (i - 2), align_bytes=64)
+            else:
+                h_grouped[i] = stage.tile([P, 2, PASSES, P, 2], F32, name="h_grouped%d" % i, tag="h_grouped", align_bytes=64)
+            for a in range(2):
+                nc.scalar.copy(out=h_grouped[i][:, a], in_=h_turned[a][:].rearrange("p g u r -> p g r u"))
+
+        def quantize_h(i):
+            h_codes[i] = stage.tile([P, 2 * PASSES * P], U32, name="h_codes%d" % i, tag="h_codes", bufs=3, align_bytes=64)
+            h_blocks[i] = stage.tile([P, 2 * PASSES * P], U8, name="h_blocks%d" % i, tag="h_blocks", bufs=3, align_bytes=64)
+            nc.vector.quantize_mx(
+                out=h_codes[i][:].bitcast(FP8X4),
+                scales=h_blocks[i][:],
+                in_=h_grouped[i][:].rearrange("p a g r u -> p (a g r u)").bitcast(BF16),
+            )
+            multiply_ahead()
+
+        def multiply_ahead():
+            while counts["multiplied"] < min(counts["drained"] + Z_BANKS, TILES * 2 * CHUNKS):
+                k = counts["multiplied"]
+                i, n, a = k // (2 * CHUNKS), k % (2 * CHUNKS) // 2, k % 2
+                if i not in h_codes or (n, PASSES - 1) not in w_codes:
+                    return
+                banks[k] = psum.tile([P, BANK], F32, name="z%d" % k, tag="z", bufs=Z_BANKS)
+                for g in range(PASSES):
+                    cols = slice((a * PASSES + g) * P, (a * PASSES + g + 1) * P)
+                    nc.tensor.matmul_mx(
+                        out=banks[k][:],
+                        lhsT=h_codes[i][:, cols].bitcast(FP8X4),
+                        lhsT_scale=h_blocks[i][:, cols],
+                        rhs=w_codes[n, g][:].bitcast(FP8X4),
+                        rhs_scale=w_blocks[n, g][:],
+                        start=(g == 0),
+                        stop=(g == PASSES - 1),
+                    )
+                counts["multiplied"] = k + 1
+
+        def drain(count=1):
+            for k in range(counts["drained"], counts["drained"] + count):
+                i, n, a = k // (2 * CHUNKS), k % (2 * CHUNKS) // 2, k % 2
+                if n == 0:
+                    t["nz", i, a] = row_tile(("zc", "zu")[a], i, ("neg_zc", "neg_zu")[a])
+                    if a == 0:
+                        stat("chunk_min", i, 2 * CHUNKS)
+                nc.vector.tensor_scalar(
+                    out=t["nz", i, a][:, n * BANK : (n + 1) * BANK], in0=banks[k][:], scalar1=-1.0, scalar2=None,
+                    op0=ALU.mult, op1=ALU.min, accum_out=t["chunk_min", i][:, a * CHUNKS + n : a * CHUNKS + n + 1],
+                )
+                counts["drained"] = k + 1
+                multiply_ahead()
+
+        def row_max(i):
+            nc.vector.tensor_reduce(
+                out=stat("neg_max", i, 2)[:], in_=t["chunk_min", i][:].rearrange("p (a n) -> p a n", a=2),
+                axis=mybir.AxisListType.X, op=ALU.min,
+            )
+
+        def max_gap(i):
+            neg_max = t["neg_max", i]
+            nc.vector.tensor_scalar(
+                out=stat("gap", i, 1)[:], in0=neg_max[:, 0:1], scalar1=neg_max[:, 1:2], scalar2=0.5,
+                op0=ALU.subtract, op1=ALU.mult,
+            )
+
+        def exp(i, a):
+            if a == 0:
+                stat("sums", i, 2)
+            t["e", i, a] = row_tile(("ec", "eu")[a], i, ("exp_c", "exp_u")[a])
+            nc.scalar.activation(
+                out=t["e", i, a][:], in_=t["nz", i, a][:], func=ACT.Exp, scale=-1.0,
+                bias=t["neg_max", i][:, a : a + 1], accum_out=t["sums", i][:, a : a + 1],
+            )
+
+        def difference(i, engine):
+            t["d", i] = rows.tile([P, V], F32, name="d%d" % i, tag="d%d" % (i % D_SLOTS), align_bytes=64)
+            engine.tensor_tensor(out=t["d", i][:], in0=t["nz", i, 1][:], in1=t["nz", i, 0][:], op=ALU.subtract)
+
+        def inverse_sums(i):
+            nc.vector.reciprocal(out=stat("inv", i, 2)[:], in_=t["sums", i][:])
+
+        def half_ratio(i):
+            nc.vector.tensor_scalar(
+                out=stat("half_r", i, 1)[:], in0=t["sums", i][:, 0:1], scalar1=t["inv", i][:, 1:2], scalar2=0.5,
+                op0=ALU.mult, op1=ALU.mult,
+            )
+
+        def log_guess(i):
+            passed = stage.tile([P, STEPS], F32, name="passed%d" % i, tag="passed", bufs=1)
+            nc.vector.tensor_scalar(
+                out=passed[:], in0=ladder[:], scalar1=t["half_r", i][:], scalar2=(0.5 - LOG_SPAN) / STEP - 0.5,
+                op0=ALU.is_le, op1=ALU.add, accum_out=stat("rung", i, 1)[:],
+            )
+
+        def coarse_shift(i):
+            nc.vector.tensor_scalar(
+                out=stat("coarse", i, 1)[:], in0=t["rung", i][:], scalar1=-0.5 * STEP, scalar2=t["gap", i][:],
+                op0=ALU.mult, op1=ALU.add,
+            )
+
+        def guess_exp(i):
+            nc.scalar.activation(out=stat("exp_neg_y", i, 1)[:], in_=t["rung", i][:], func=ACT.Exp, scale=-STEP, bias=0.5)
+
+        def guess_square(i):
+            nc.scalar.activation(out=stat("fine", i, 1)[:], in_=t["exp_neg_y", i][:], func=ACT.Square, scale=t["half_r", i][:], bias=-1.0)
+
+        def shift(i):
+            nc.scalar.activation(out=stat("shift", i, 1)[:], in_=t["fine", i][:], func=ACT.Identity, bias=t["coarse", i][:])
+
+        def tanh(i):
+            t["u", i] = row_tile("zu", i, "u")
+            nc.scalar.activation(out=t["u", i][:], in_=t["d", i][:], func=ACT.Tanh, scale=0.5, bias=t["shift", i][:])
+
+        def log(i, a):
+            if a == 0:
+                t["log", i, 0] = stage.tile([P, V], F32, name="log_plus%d" % i, tag="log_plus")
+            else:
+                t["log", i, 1] = t["u", i]
+            nc.scalar.activation(out=t["log", i, a][:], in_=t["u", i][:], func=ACT.Ln, scale=(SHRINK, -SHRINK)[a], bias=1.0)
+
+        def kl(i, a):
+            if a == 0:
+                stat("kl", i, 2)
+            nc.vector.scalar_tensor_tensor(
+                out=t["log", i, a][:], in0=t["log", i, a][:], scalar=t["inv", i][:, a : a + 1], in1=t["e", i, a][:],
+                op0=ALU.mult, op1=ALU.mult, accum_out=t["kl", i][:, a : a + 1],
+            )
+
+        def weight(i):
+            nc.vector.tensor_scalar(
+                out=stat("a", i, 1)[:], in0=t["kl", i][:, 0:1], scalar1=t["kl", i][:, 1:2], scalar2=0.5 / LN2,
+                op0=ALU.add, op1=ALU.mult,
+            )
+
+        def combine(i, parts=1):
+            result = row_tile("ec", i, "result")
+            for s in range(parts):
+                cols = slice(s * V // parts, (s + 1) * V // parts)
+                nc.vector.scalar_tensor_tensor(
+                    out=result[:, cols], in0=t["d", i][:, cols], scalar=t["a", i][:], in1=t["nz", i, 0][:, cols],
+                    op0=ALU.mult, op1=ALU.subtract,
+                )
+                nc.sync.dma_start(out=out[i * P : (i + 1) * P, cols], in_=result[:, cols])
+
+        def guess(i, first=None, second=None, third=None):
+            for step, between in ((inverse_sums, first), (half_ratio, second), (log_guess, third), (coarse_shift, None)):
+                step(i)
+                if between is not None:
+                    between()
+
+        nc.sync.dma_start(out=scale[:], in_=w_scale.rearrange("(g p t) o -> p g (t o)", p=P, t=PACK))
+        load_w(0)
+        load_w(1)
+        load_h(0)
+        load_w(2)
+        load_w(3)
+        load_h(1)
+        make_identity(nc, identity[:])
+        nc.gpsimd.iota(ladder[:], pattern=[[1, STEPS]], base=0, channel_multiplier=0, allow_small_or_imprecise_dtypes=True)
+        nc.scalar.activation(out=ladder[:], in_=ladder[:], func=ACT.Exp, scale=STEP, bias=-LOG_SPAN - LN2)
+        turn(0)
+        for j in range(len(pieces)):
+            widen(j, 2 if j < 2 else 0)
+            if j == 2 or j == 4:
+                regroup(j // 2 - 1)
+                turn(j // 2)
+            interleave(j, nc.scalar.copy if j == 7 else nc.vector.tensor_copy)
+            if j in (4, 6):
+                drain(2)
+            if j in (3, 5):
+                quantize_w(j - 1)
+                quantize_w(j)
+            if j == 1:
+                quantize_w(0)
+            if j == 2:
+                quantize_w(1)
+                quantize_h(0)
+        regroup(2)
+        turn(3)
+        quantize_w(6)
+        quantize_h(1)
+        drain(2)
+        quantize_w(7)
+        quantize_h(2)
+        regroup(3)
+        drain(2)
+        row_max(0)
+        difference(0, nc.gpsimd)
+        exp(0, 0)
+        exp(0, 1)
+        drain(4)
+        turn(4)
+        drain(4)
+        row_max(1)
+        exp(1, 0)
+        guess(0, lambda: max_gap(0), lambda: max_gap(1), lambda: quantize_h(3))
+        difference(1, nc.gpsimd)
+        guess_exp(0)
+        exp(1, 1)
+        guess_square(0)
+        regroup(4)
+        shift(0)
+        drain(8)
+        turn(5)
+        row_max(2)
+        tanh(0)
+        guess(1, lambda: max_gap(2), None, lambda: quantize_h(4))
+        difference(2, nc.gpsimd)
+        exp(2, 0)
+        guess_exp(1)
+        exp(2, 1)
+        guess_square(1)
+        shift(1)
+        tanh(1)
+        drain(8)
+        row_max(3)
+        guess(2, lambda: max_gap(3))
+        guess_exp(2)
+        guess_square(2)
+        shift(2)
+        tanh(2)
+        log(0, 0)
+        log(0, 1)
+        regroup(5)
+        kl(0, 0)
+        kl(0, 1)
+        quantize_h(5)
+        weight(0)
+        combine(0)
+        turn(6)
+        difference(3, nc.gpsimd)
+        drain(8)
+        row_max(4)
+        log(1, 0)
+        log(1, 1)
+        log(2, 0)
+        log(2, 1)
+        regroup(6)
+        kl(1, 0)
+        kl(1, 1)
+        quantize_h(6)
+        weight(1)
+        exp(3, 0)
+        exp(3, 1)
+        guess(3, lambda: max_gap(4))
+        combine(1)
+        difference(4, nc.gpsimd)
+        drain(8)
+        turn(7)
+        row_max(5)
+        exp(4, 0)
+        guess_exp(3)
+        exp(4, 1)
+        guess_square(3)
+        shift(3)
+        tanh(3)
+        guess(4, lambda: max_gap(5), None, lambda: kl(2, 0))
+        exp(5, 0)
+        guess_exp(4)
+        exp(5, 1)
+        guess_square(4)
+        kl(2, 1)
+        weight(2)
+        guess(5)
+        combine(2)
+        difference(5, nc.vector)
+        shift(4)
+        tanh(4)
+        guess_exp(5)
+        guess_square(5)
+        regroup(7)
+        shift(5)
+        tanh(5)
+        quantize_h(7)
+        drain(8)
+        row_max(6)
+        log(3, 0)
+        log(3, 1)
+        kl(3, 0)
+        kl(3, 1)
+        max_gap(6)
+        weight(3)
+        combine(3)
+        difference(6, nc.gpsimd)
+        drain(8)
+        row_max(7)
+        log(4, 0)
+        log(4, 1)
+        log(5, 0)
+        log(5, 1)
+        kl(4, 0)
+        exp(6, 0)
+        exp(6, 1)
+        guess(6, lambda: max_gap(7), None, lambda: kl(4, 1))
+        exp(7, 0)
+        weight(4)
+        guess_exp(6)
+        exp(7, 1)
+        guess_square(6)
+        shift(6)
+        tanh(6)
+        combine(4)
+        guess(7, None, None, lambda: difference(7, nc.vector))
+        guess_exp(7)
+        guess_square(7)
+        shift(7)
+        tanh(7)
+        kl(5, 0)
+        kl(5, 1)
+        weight(5)
+        combine(5)
+        log(6, 0)
+        log(6, 1)
+        kl(6, 0)
+        kl(6, 1)
+        log(7, 0)
+        log(7, 1)
+        weight(6)
+        kl(7, 0)
+        combine(6)
+        kl(7, 1)
+        weight(7)
+        combine(7, 4)

@@ -22,14 +22,15 @@ PASSES = D // (P * PACK)
 BANK = 512
 CHUNKS = V // BANK
 TILES = N // P
+Z_SLOTS = 5
 SLOTS = 4
-D_SLOTS = 3
 Z_BANKS = 6
 LN2 = math.log(2.0)
 SHRINK = 1.0 - 2.0**-24
 STEPS = 256
 LOG_SPAN = math.log(V)
 STEP = 2.0 * LOG_SPAN / STEPS
+GUESS_TOP = LOG_SPAN + STEP / 2.0
 
 
 def tile_adacadjsdcontrastlogits_kernel(tc, hc, hu, w_bytes, w_scale, out):
@@ -49,7 +50,8 @@ def tile_adacadjsdcontrastlogits_kernel(tc, hc, hu, w_bytes, w_scale, out):
         counts = {"multiplied": 0, "drained": 0}
 
         def row_tile(role, i, name):
-            return rows.tile([P, V], F32, name="%s%d" % (name, i), tag="%s%d" % (role, i % SLOTS), align_bytes=64)
+            slot = i % (Z_SLOTS if role in ("zc", "zu") else SLOTS)
+            return rows.tile([P, V], F32, name="%s%d" % (name, i), tag="%s%d" % (role, slot), align_bytes=64)
 
         def stat(name, i, width):
             t[name, i] = keep.tile([P, width], F32, name="%s%d" % (name, i))
@@ -62,7 +64,7 @@ def tile_adacadjsdcontrastlogits_kernel(tc, hc, hu, w_bytes, w_scale, out):
 
         def load_w(j):
             n, g = pieces[j]
-            w_raw[j] = stage.tile([P, PACK, BANK], U8, name="w_raw%d" % j, tag="w_raw", bufs=4)
+            w_raw[j] = rows.tile([P, PACK, BANK], U8, name="w_raw%d" % j, tag="%s%d" % (("zc", "zu")[j % 2], 1 + j // 2), align_bytes=64)
             nc.sync.dma_start(out=w_raw[j][:], in_=w_view[g][:, :, n * BANK : (n + 1) * BANK])
 
         def load_h(i):
@@ -72,14 +74,12 @@ def tile_adacadjsdcontrastlogits_kernel(tc, hc, hu, w_bytes, w_scale, out):
 
         def widen(j, on_vector=0):
             g = pieces[j][1]
-            w_planes[j] = rows.tile([P, PACK, BANK], BF16, name="w_planes%d" % j, tag=("ec3", "eu3", "zc3")[j % 3], align_bytes=64)
+            w_planes[j] = rows.tile([P, PACK, BANK], BF16, name="w_planes%d" % j, tag=("ec3", "eu3", "ec1")[j % 3], align_bytes=64)
             for k in range(PACK):
                 if k < on_vector:
                     nc.vector.tensor_scalar(out=w_planes[j][:, k, :], in0=w_raw[j][:, k, :].bitcast(FP8), scalar1=scale[:, g, k : k + 1], scalar2=None, op0=ALU.mult)
                 else:
                     nc.scalar.activation(out=w_planes[j][:, k, :], in_=w_raw[j][:, k, :].bitcast(FP8), func=ACT.Copy, scale=scale[:, g, k : k + 1])
-            if j + 4 < len(pieces):
-                load_w(j + 4)
 
         def interleave(j, copy):
             w_grouped[j] = rows.tile([P, BANK, PACK], BF16, name="w_grouped%d" % j, tag=("ec2", "eu2")[j % 2], align_bytes=64)
@@ -108,13 +108,13 @@ def tile_adacadjsdcontrastlogits_kernel(tc, hc, hu, w_bytes, w_scale, out):
             if i + 2 < TILES:
                 load_h(i + 2)
 
-        def regroup(i):
-            if 2 <= i < 2 + D_SLOTS:
-                h_grouped[i] = rows.tile([P, 2, PASSES, P, 2], F32, name="h_grouped%d" % i, tag="d%d" % (i - 2), align_bytes=64)
+        def regroup(i, copy, slot=None):
+            if slot is not None:
+                h_grouped[i] = rows.tile([P, 2, PASSES, P, 2], F32, name="h_grouped%d" % i, tag="d%d" % slot, align_bytes=64)
             else:
-                h_grouped[i] = stage.tile([P, 2, PASSES, P, 2], F32, name="h_grouped%d" % i, tag="h_grouped", align_bytes=64)
+                h_grouped[i] = stage.tile([P, 2, PASSES, P, 2], F32, name="h_grouped%d" % i, tag="h_grouped", bufs=1, align_bytes=64)
             for a in range(2):
-                nc.scalar.copy(out=h_grouped[i][:, a], in_=h_turned[a][:].rearrange("p g u r -> p g r u"))
+                copy(out=h_grouped[i][:, a], in_=h_turned[a][:].rearrange("p g u r -> p g r u"))
 
         def quantize_h(i):
             h_codes[i] = stage.tile([P, 2 * PASSES * P], U32, name="h_codes%d" % i, tag="h_codes", bufs=3, align_bytes=64)
@@ -126,11 +126,14 @@ def tile_adacadjsdcontrastlogits_kernel(tc, hc, hu, w_bytes, w_scale, out):
             )
             multiply_ahead()
 
+        def chunk(k):
+            return k // (2 * CHUNKS), k % (2 * CHUNKS) // 2, k % 2
+
         def multiply_ahead():
             while counts["multiplied"] < min(counts["drained"] + Z_BANKS, TILES * 2 * CHUNKS):
                 k = counts["multiplied"]
-                i, n, a = k // (2 * CHUNKS), k % (2 * CHUNKS) // 2, k % 2
-                if i not in h_codes or (n, PASSES - 1) not in w_codes:
+                i, n, a = chunk(k)
+                if i not in h_codes or any((n, g) not in w_codes for g in range(PASSES)):
                     return
                 banks[k] = psum.tile([P, BANK], F32, name="z%d" % k, tag="z", bufs=Z_BANKS)
                 for g in range(PASSES):
@@ -148,7 +151,7 @@ def tile_adacadjsdcontrastlogits_kernel(tc, hc, hu, w_bytes, w_scale, out):
 
         def drain(count=1):
             for k in range(counts["drained"], counts["drained"] + count):
-                i, n, a = k // (2 * CHUNKS), k % (2 * CHUNKS) // 2, k % 2
+                i, n, a = chunk(k)
                 if n == 0:
                     t["nz", i, a] = row_tile(("zc", "zu")[a], i, ("neg_zc", "neg_zu")[a])
                     if a == 0:
@@ -169,8 +172,8 @@ def tile_adacadjsdcontrastlogits_kernel(tc, hc, hu, w_bytes, w_scale, out):
         def max_gap(i):
             neg_max = t["neg_max", i]
             nc.vector.tensor_scalar(
-                out=stat("gap", i, 1)[:], in0=neg_max[:, 0:1], scalar1=neg_max[:, 1:2], scalar2=0.5,
-                op0=ALU.subtract, op1=ALU.mult,
+                out=stat("gap", i, 1)[:], in0=neg_max[:, 0:1], scalar1=neg_max[:, 1:2], scalar2=GUESS_TOP - 0.5,
+                op0=ALU.subtract, op1=ALU.add,
             )
 
         def exp(i, a):
@@ -182,64 +185,55 @@ def tile_adacadjsdcontrastlogits_kernel(tc, hc, hu, w_bytes, w_scale, out):
                 bias=t["neg_max", i][:, a : a + 1], accum_out=t["sums", i][:, a : a + 1],
             )
 
-        def difference(i, engine):
-            t["d", i] = rows.tile([P, V], F32, name="d%d" % i, tag="d%d" % (i % D_SLOTS), align_bytes=64)
+        def difference(i, engine, slot):
+            t["d", i] = rows.tile([P, V], F32, name="d%d" % i, tag="d%d" % slot, align_bytes=64)
             engine.tensor_tensor(out=t["d", i][:], in0=t["nz", i, 1][:], in1=t["nz", i, 0][:], op=ALU.subtract)
 
         def inverse_sums(i):
             nc.vector.reciprocal(out=stat("inv", i, 2)[:], in_=t["sums", i][:])
 
-        def half_ratio(i):
-            nc.vector.tensor_scalar(
-                out=stat("half_r", i, 1)[:], in0=t["sums", i][:, 0:1], scalar1=t["inv", i][:, 1:2], scalar2=0.5,
-                op0=ALU.mult, op1=ALU.mult,
-            )
-
-        def log_guess(i):
+        def ladder_count(i):
             passed = stage.tile([P, STEPS], F32, name="passed%d" % i, tag="passed", bufs=1)
-            nc.vector.tensor_scalar(
-                out=passed[:], in0=ladder[:], scalar1=t["half_r", i][:], scalar2=(0.5 - LOG_SPAN) / STEP - 0.5,
-                op0=ALU.is_le, op1=ALU.add, accum_out=stat("rung", i, 1)[:],
+            nc.vector.scalar_tensor_tensor(
+                out=passed[:], in0=ladder[:], scalar=t["sums", i][:, 1:2], in1=t["sums", i][:, 0:1].to_broadcast([P, STEPS]),
+                op0=ALU.mult, op1=ALU.is_le, accum_out=stat("count", i, 1)[:],
             )
 
-        def coarse_shift(i):
-            nc.vector.tensor_scalar(
-                out=stat("coarse", i, 1)[:], in0=t["rung", i][:], scalar1=-0.5 * STEP, scalar2=t["gap", i][:],
-                op0=ALU.mult, op1=ALU.add,
-            )
-
-        def guess_exp(i):
-            nc.scalar.activation(out=stat("exp_neg_y", i, 1)[:], in_=t["rung", i][:], func=ACT.Exp, scale=-STEP, bias=0.5)
+        def guess_terms(i):
+            nc.scalar.activation(out=stat("half_exp", i, 1)[:], in_=t["count", i][:], func=ACT.Exp, scale=-STEP, bias=GUESS_TOP - LN2)
+            nc.scalar.activation(out=stat("ratio", i, 1)[:], in_=t["sums", i][:, 0:1], func=ACT.Copy, scale=t["inv", i][:, 1:2])
+            nc.scalar.activation(out=stat("coarse", i, 1)[:], in_=t["count", i][:], func=ACT.Identity, scale=-STEP, bias=t["gap", i][:])
 
         def guess_square(i):
-            nc.scalar.activation(out=stat("fine", i, 1)[:], in_=t["exp_neg_y", i][:], func=ACT.Square, scale=t["half_r", i][:], bias=-1.0)
+            nc.scalar.activation(out=stat("fine", i, 1)[:], in_=t["half_exp", i][:], func=ACT.Square, scale=t["ratio", i][:], bias=-1.0)
 
         def shift(i):
-            nc.scalar.activation(out=stat("shift", i, 1)[:], in_=t["fine", i][:], func=ACT.Identity, bias=t["coarse", i][:])
+            nc.scalar.activation(out=stat("shift", i, 1)[:], in_=t["coarse", i][:], func=ACT.Identity, scale=0.5, bias=t["fine", i][:])
 
         def tanh(i):
             t["u", i] = row_tile("zu", i, "u")
             nc.scalar.activation(out=t["u", i][:], in_=t["d", i][:], func=ACT.Tanh, scale=0.5, bias=t["shift", i][:])
 
-        def log(i, a):
-            if a == 0:
+        def log(i, a, part=0, parts=1):
+            cols = slice(part * V // parts, (part + 1) * V // parts)
+            if a == 0 and part == 0:
                 t["log", i, 0] = stage.tile([P, V], F32, name="log_plus%d" % i, tag="log_plus")
-            else:
                 t["log", i, 1] = t["u", i]
-            nc.scalar.activation(out=t["log", i, a][:], in_=t["u", i][:], func=ACT.Ln, scale=(SHRINK, -SHRINK)[a], bias=1.0)
+            nc.scalar.activation(out=t["log", i, a][:, cols], in_=t["u", i][:, cols], func=ACT.Ln, scale=(SHRINK, -SHRINK)[a], bias=1.0)
 
-        def kl(i, a):
-            if a == 0:
-                stat("kl", i, 2)
+        def kl(i, a, part=0, parts=1):
+            cols = slice(part * V // parts, (part + 1) * V // parts)
+            if a == 0 and part == 0:
+                stat("kl", i, 2 * parts)
             nc.vector.scalar_tensor_tensor(
-                out=t["log", i, a][:], in0=t["log", i, a][:], scalar=t["inv", i][:, a : a + 1], in1=t["e", i, a][:],
-                op0=ALU.mult, op1=ALU.mult, accum_out=t["kl", i][:, a : a + 1],
+                out=t["log", i, a][:, cols], in0=t["log", i, a][:, cols], scalar=t["inv", i][:, a : a + 1], in1=t["e", i, a][:, cols],
+                op0=ALU.mult, op1=ALU.mult, accum_out=t["kl", i][:, 2 * part + a : 2 * part + a + 1],
             )
 
         def weight(i):
             nc.vector.tensor_scalar(
-                out=stat("a", i, 1)[:], in0=t["kl", i][:, 0:1], scalar1=t["kl", i][:, 1:2], scalar2=0.5 / LN2,
-                op0=ALU.add, op1=ALU.mult,
+                out=t["kl", i][:], in0=t["kl", i][:], scalar1=0.5 / LN2, scalar2=None,
+                op0=ALU.mult, op1=ALU.add, accum_out=stat("a", i, 1)[:],
             )
 
         def combine(i, parts=1):
@@ -252,182 +246,191 @@ def tile_adacadjsdcontrastlogits_kernel(tc, hc, hu, w_bytes, w_scale, out):
                 )
                 nc.sync.dma_start(out=out[i * P : (i + 1) * P, cols], in_=result[:, cols])
 
-        def guess(i, first=None, second=None, third=None):
-            for step, between in ((inverse_sums, first), (half_ratio, second), (log_guess, third), (coarse_shift, None)):
-                step(i)
-                if between is not None:
-                    between()
+        def guess(i):
+            inverse_sums(i)
+            max_gap(i)
+            ladder_count(i)
 
         nc.sync.dma_start(out=scale[:], in_=w_scale.rearrange("(g p t) o -> p g (t o)", p=P, t=PACK))
         load_w(0)
         load_w(1)
         load_h(0)
-        load_w(2)
-        load_w(3)
+        for j in range(2, len(pieces)):
+            load_w(j)
         load_h(1)
         make_identity(nc, identity[:])
         nc.gpsimd.iota(ladder[:], pattern=[[1, STEPS]], base=0, channel_multiplier=0, allow_small_or_imprecise_dtypes=True)
-        nc.scalar.activation(out=ladder[:], in_=ladder[:], func=ACT.Exp, scale=STEP, bias=-LOG_SPAN - LN2)
+        nc.scalar.activation(out=ladder[:], in_=ladder[:], func=ACT.Exp, scale=STEP, bias=-LOG_SPAN)
         turn(0)
-        for j in range(len(pieces)):
+        for j in range(6):
             widen(j, 2 if j < 2 else 0)
-            if j == 2 or j == 4:
-                regroup(j // 2 - 1)
-                turn(j // 2)
-            interleave(j, nc.scalar.copy if j == 7 else nc.vector.tensor_copy)
-            if j in (4, 6):
-                drain(2)
-            if j in (3, 5):
-                quantize_w(j - 1)
-                quantize_w(j)
-            if j == 1:
-                quantize_w(0)
             if j == 2:
-                quantize_w(1)
+                regroup(0, nc.scalar.copy)
+                turn(1)
+            interleave(j, nc.vector.tensor_copy)
+            if j > 0:
+                quantize_w(j - 1)
+            if j == 2:
                 quantize_h(0)
-        regroup(2)
-        turn(3)
-        quantize_w(6)
-        quantize_h(1)
+            if j == 4:
+                drain(2)
+        widen(6)
+        widen(7)
+        drain(2)
+        quantize_w(5)
+        interleave(6, nc.scalar.copy)
+        interleave(7, nc.vector.tensor_copy)
+        regroup(1, nc.scalar.copy)
+        turn(2)
         drain(2)
         quantize_w(7)
-        quantize_h(2)
-        regroup(3)
+        quantize_w(6)
+        regroup(2, nc.scalar.copy, 0)
+        quantize_h(1)
+        turn(3)
         drain(2)
         row_max(0)
-        difference(0, nc.gpsimd)
+        quantize_h(2)
+        difference(0, nc.gpsimd, 0)
         exp(0, 0)
         exp(0, 1)
+        regroup(3, nc.scalar.copy, 1)
         drain(4)
         turn(4)
         drain(4)
         row_max(1)
         exp(1, 0)
-        guess(0, lambda: max_gap(0), lambda: max_gap(1), lambda: quantize_h(3))
-        difference(1, nc.gpsimd)
-        guess_exp(0)
+        guess(0)
+        quantize_h(3)
+        difference(1, nc.gpsimd, 1)
+        guess_terms(0)
         exp(1, 1)
         guess_square(0)
-        regroup(4)
+        regroup(4, nc.scalar.copy, 2)
         shift(0)
         drain(8)
         turn(5)
         row_max(2)
         tanh(0)
-        guess(1, lambda: max_gap(2), None, lambda: quantize_h(4))
-        difference(2, nc.gpsimd)
+        guess(1)
+        quantize_h(4)
+        difference(2, nc.gpsimd, 2)
         exp(2, 0)
-        guess_exp(1)
+        guess_terms(1)
         exp(2, 1)
         guess_square(1)
+        drain(4)
+        regroup(5, nc.vector.tensor_copy, 3)
+        drain(4)
         shift(1)
         tanh(1)
-        drain(8)
+        turn(6)
         row_max(3)
-        guess(2, lambda: max_gap(3))
-        guess_exp(2)
+        guess(2)
+        quantize_h(5)
+        difference(3, nc.gpsimd, 3)
+        guess_terms(2)
         guess_square(2)
         shift(2)
         tanh(2)
+        drain(4)
+        regroup(6, nc.vector.tensor_copy)
+        drain(4)
+        row_max(4)
+        turn(7)
         log(0, 0)
         log(0, 1)
-        regroup(5)
+        quantize_h(6)
         kl(0, 0)
         kl(0, 1)
-        quantize_h(5)
-        weight(0)
-        combine(0)
-        turn(6)
-        difference(3, nc.gpsimd)
-        drain(8)
-        row_max(4)
         log(1, 0)
         log(1, 1)
         log(2, 0)
         log(2, 1)
-        regroup(6)
         kl(1, 0)
+        weight(0)
         kl(1, 1)
-        quantize_h(6)
+        combine(0)
         weight(1)
+        regroup(7, nc.vector.tensor_copy, 0)
+        combine(1)
+        difference(4, nc.gpsimd, 1)
+        drain(8)
+        row_max(5)
         exp(3, 0)
         exp(3, 1)
-        guess(3, lambda: max_gap(4))
-        combine(1)
-        difference(4, nc.gpsimd)
-        drain(8)
-        turn(7)
-        row_max(5)
         exp(4, 0)
-        guess_exp(3)
         exp(4, 1)
-        guess_square(3)
-        shift(3)
-        tanh(3)
-        guess(4, lambda: max_gap(5), None, lambda: kl(2, 0))
         exp(5, 0)
-        guess_exp(4)
-        exp(5, 1)
-        guess_square(4)
-        kl(2, 1)
-        weight(2)
-        guess(5)
-        combine(2)
-        difference(5, nc.vector)
-        shift(4)
-        tanh(4)
-        guess_exp(5)
-        guess_square(5)
-        regroup(7)
-        shift(5)
-        tanh(5)
+        guess(3)
+        guess(4)
         quantize_h(7)
+        difference(5, nc.gpsimd, 0)
         drain(8)
         row_max(6)
+        guess_terms(3)
+        guess_terms(4)
+        exp(5, 1)
+        guess_square(3)
+        guess_square(4)
+        shift(3)
+        shift(4)
+        tanh(3)
+        guess(5)
+        kl(2, 0)
+        kl(2, 1)
+        guess_terms(5)
+        tanh(4)
+        guess_square(5)
+        shift(5)
+        tanh(5)
+        weight(2)
+        combine(2)
+        difference(6, nc.gpsimd, 2)
+        drain(8)
+        row_max(7)
         log(3, 0)
         log(3, 1)
         kl(3, 0)
         kl(3, 1)
-        max_gap(6)
-        weight(3)
-        combine(3)
-        difference(6, nc.gpsimd)
-        drain(8)
-        row_max(7)
         log(4, 0)
         log(4, 1)
         log(5, 0)
         log(5, 1)
+        weight(3)
+        combine(3)
         kl(4, 0)
+        kl(4, 1)
+        difference(7, nc.vector, 3)
+        weight(4)
         exp(6, 0)
         exp(6, 1)
-        guess(6, lambda: max_gap(7), None, lambda: kl(4, 1))
+        guess(6)
+        combine(4)
+        kl(5, 0)
         exp(7, 0)
-        weight(4)
-        guess_exp(6)
+        guess_terms(6)
         exp(7, 1)
         guess_square(6)
         shift(6)
+        guess(7)
+        kl(5, 1)
         tanh(6)
-        combine(4)
-        guess(7, None, None, lambda: difference(7, nc.vector))
-        guess_exp(7)
+        guess_terms(7)
         guess_square(7)
         shift(7)
         tanh(7)
-        kl(5, 0)
-        kl(5, 1)
         weight(5)
         combine(5)
-        log(6, 0)
-        log(6, 1)
-        kl(6, 0)
-        kl(6, 1)
+        for part in range(2):
+            for a in range(2):
+                log(6, a, part, 2)
+                kl(6, a, part, 2)
         log(7, 0)
         log(7, 1)
         weight(6)
+        combine(6, 2)
         kl(7, 0)
-        combine(6)
         kl(7, 1)
         weight(7)
         combine(7, 4)

@@ -22,9 +22,11 @@ PASSES = D // (P * PACK)
 BANK = 512
 CHUNKS = V // BANK
 TILES = N // P
-Z_SLOTS = 5
-SLOTS = 4
+BANKS_PER_TILE = 2 * CHUNKS
 Z_BANKS = 6
+Z_SLOTS = 5
+E_SLOTS = 4
+
 LN2 = math.log(2.0)
 SHRINK = 1.0 - 2.0**-24
 STEPS = 256
@@ -42,50 +44,51 @@ def tile_adacadjsdcontrastlogits_kernel(tc, hc, hu, w_bytes, w_scale, out):
         psum = ctx.enter_context(tc.psum_pool(name="psum", bufs=1))
         ctx.enter_context(tc.manual_schedule())
 
-        w_view = w_bytes.rearrange("(g p t) n -> g p t n", p=P, t=PACK)
         pieces = [(n, g) for n in range(CHUNKS) for g in range(PASSES)]
+        w_view = w_bytes.rearrange("(g p t) n -> g p t n", p=P, t=PACK)
         w_raw, w_planes, w_grouped, w_codes, w_blocks = {}, {}, {}, {}, {}
         h_raw, h_turned, h_grouped, h_codes, h_blocks = {}, {}, {}, {}, {}
-        banks, t = {}, {}
+        banks, neg_z, exps, diff, tanh_u, logs, stats = {}, {}, {}, {}, {}, {}, {}
         counts = {"multiplied": 0, "drained": 0}
 
-        def row_tile(role, i, name):
-            slot = i % (Z_SLOTS if role in ("zc", "zu") else SLOTS)
-            return rows.tile([P, V], F32, name="%s%d" % (name, i), tag="%s%d" % (role, slot), align_bytes=64)
+        def buffer(tag, shape, dtype, name):
+            return rows.tile(shape, dtype, name=name, tag=tag, align_bytes=64)
+
+        def z_tag(i, a):
+            return "z%d_%d" % (a, i % Z_SLOTS)
+
+        def e_tag(i, a):
+            return "e%d_%d" % (a, i % E_SLOTS)
 
         def stat(name, i, width):
-            t[name, i] = keep.tile([P, width], F32, name="%s%d" % (name, i))
-            return t[name, i]
+            stats[name, i] = keep.tile([P, width], F32, name="%s%d" % (name, i))
+            return stats[name, i]
 
         scale = keep.tile([P, PASSES, PACK], F32, name="scale")
         identity = keep.tile([P, P], F32, name="identity")
-
         ladder = keep.tile([P, STEPS], F32, name="ladder")
 
         def load_w(j):
             n, g = pieces[j]
-            w_raw[j] = rows.tile([P, PACK, BANK], U8, name="w_raw%d" % j, tag="%s%d" % (("zc", "zu")[j % 2], 1 + j // 2), align_bytes=64)
+            w_raw[j] = buffer(z_tag(1 + j // 2, j % 2), [P, PACK, BANK], U8, "w_raw%d" % j)
             nc.sync.dma_start(out=w_raw[j][:], in_=w_view[g][:, :, n * BANK : (n + 1) * BANK])
-
-        def load_h(i):
-            for a, h in enumerate((hc, hu)):
-                h_raw[i, a] = stage.tile([P, D], BF16, name="h_raw%d_%d" % (i, a), tag="h_raw%d" % a)
-                nc.sync.dma_start(out=h_raw[i, a][:], in_=h[i * P : (i + 1) * P, :])
 
         def widen(j, on_vector=0):
             g = pieces[j][1]
-            w_planes[j] = rows.tile([P, PACK, BANK], BF16, name="w_planes%d" % j, tag=("ec3", "eu3", "ec1")[j % 3], align_bytes=64)
-            for k in range(PACK):
-                if k < on_vector:
-                    nc.vector.tensor_scalar(out=w_planes[j][:, k, :], in0=w_raw[j][:, k, :].bitcast(FP8), scalar1=scale[:, g, k : k + 1], scalar2=None, op0=ALU.mult)
+            tag = (e_tag(3, 0), e_tag(3, 1), e_tag(1, 0))[j % 3]
+            w_planes[j] = buffer(tag, [P, PACK, BANK], BF16, "w_planes%d" % j)
+            for t in range(PACK):
+                codes, factor = w_raw[j][:, t, :].bitcast(FP8), scale[:, g, t : t + 1]
+                if t < on_vector:
+                    nc.vector.tensor_scalar(out=w_planes[j][:, t, :], in0=codes, scalar1=factor, scalar2=None, op0=ALU.mult)
                 else:
-                    nc.scalar.activation(out=w_planes[j][:, k, :], in_=w_raw[j][:, k, :].bitcast(FP8), func=ACT.Copy, scale=scale[:, g, k : k + 1])
+                    nc.scalar.activation(out=w_planes[j][:, t, :], in_=codes, func=ACT.Copy, scale=factor)
 
         def interleave(j, copy):
-            w_grouped[j] = rows.tile([P, BANK, PACK], BF16, name="w_grouped%d" % j, tag=("ec2", "eu2")[j % 2], align_bytes=64)
+            w_grouped[j] = buffer(e_tag(2, j % 2), [P, BANK, PACK], BF16, "w_grouped%d" % j)
             copy(
-                out=w_grouped[j][:].rearrange("p (c i) t -> p c t i", i=4),
-                in_=w_planes[j][:].rearrange("p t (c i) -> p c t i", i=4),
+                out=w_grouped[j][:].rearrange("p (c x) t -> p c t x", x=4),
+                in_=w_planes[j][:].rearrange("p t (c x) -> p c t x", x=4),
             )
 
         def quantize_w(j):
@@ -94,27 +97,33 @@ def tile_adacadjsdcontrastlogits_kernel(tc, hc, hu, w_bytes, w_scale, out):
             nc.vector.quantize_mx(
                 out=w_codes[pieces[j]][:].bitcast(FP8X4),
                 scales=w_blocks[pieces[j]][:],
-                in_=w_grouped[j][:].rearrange("p n t -> p (n t)"),
+                in_=w_grouped[j][:].rearrange("p c t -> p (c t)"),
             )
             multiply_ahead()
+
+        def load_h(i):
+            for a, h in enumerate((hc, hu)):
+                h_raw[i, a] = stage.tile([P, D], BF16, name="h_raw%d_%d" % (i, a), tag="h_raw%d" % a)
+                nc.sync.dma_start(out=h_raw[i, a][:], in_=h[i * P : (i + 1) * P, :])
 
         def turn(i):
             for a in range(2):
                 words = h_raw[i, a][:].bitcast(F32)
                 h_turned[a] = psum.tile([P, PASSES, 2, P], F32, name="h_turned%d_%d" % (i, a), tag="h_turned%d" % a)
                 for g in range(PASSES):
-                    for u in range(2):
-                        nc.tensor.transpose(h_turned[a][:, g, u, :], words[:, 256 * g + u : 256 * (g + 1) : 2], identity[:])
+                    for v in range(2):
+                        nc.tensor.transpose(h_turned[a][:, g, v, :], words[:, 256 * g + v : 256 * (g + 1) : 2], identity[:])
             if i + 2 < TILES:
                 load_h(i + 2)
 
-        def regroup(i, copy, slot=None):
-            if slot is not None:
-                h_grouped[i] = rows.tile([P, 2, PASSES, P, 2], F32, name="h_grouped%d" % i, tag="d%d" % slot, align_bytes=64)
+        def regroup(i, copy, d_slot=None):
+            shape, name = [P, 2, PASSES, P, 2], "h_grouped%d" % i
+            if d_slot is None:
+                h_grouped[i] = stage.tile(shape, F32, name=name, tag="h_grouped", bufs=1, align_bytes=64)
             else:
-                h_grouped[i] = stage.tile([P, 2, PASSES, P, 2], F32, name="h_grouped%d" % i, tag="h_grouped", bufs=1, align_bytes=64)
+                h_grouped[i] = buffer("d%d" % d_slot, shape, F32, name)
             for a in range(2):
-                copy(out=h_grouped[i][:, a], in_=h_turned[a][:].rearrange("p g u r -> p g r u"))
+                copy(out=h_grouped[i][:, a], in_=h_turned[a][:].rearrange("p g v r -> p g r v"))
 
         def quantize_h(i):
             h_codes[i] = stage.tile([P, 2 * PASSES * P], U32, name="h_codes%d" % i, tag="h_codes", bufs=3, align_bytes=64)
@@ -122,148 +131,158 @@ def tile_adacadjsdcontrastlogits_kernel(tc, hc, hu, w_bytes, w_scale, out):
             nc.vector.quantize_mx(
                 out=h_codes[i][:].bitcast(FP8X4),
                 scales=h_blocks[i][:],
-                in_=h_grouped[i][:].rearrange("p a g r u -> p (a g r u)").bitcast(BF16),
+                in_=h_grouped[i][:].rearrange("p a g r v -> p (a g r v)").bitcast(BF16),
             )
             multiply_ahead()
 
-        def chunk(k):
-            return k // (2 * CHUNKS), k % (2 * CHUNKS) // 2, k % 2
+        def bank_index(b):
+            return b // BANKS_PER_TILE, b % BANKS_PER_TILE // 2, b % 2
 
         def multiply_ahead():
-            while counts["multiplied"] < min(counts["drained"] + Z_BANKS, TILES * 2 * CHUNKS):
-                k = counts["multiplied"]
-                i, n, a = chunk(k)
+            while counts["multiplied"] < min(counts["drained"] + Z_BANKS, TILES * BANKS_PER_TILE):
+                b = counts["multiplied"]
+                i, n, a = bank_index(b)
                 if i not in h_codes or any((n, g) not in w_codes for g in range(PASSES)):
                     return
-                banks[k] = psum.tile([P, BANK], F32, name="z%d" % k, tag="z", bufs=Z_BANKS)
+                banks[b] = psum.tile([P, BANK], F32, name="z%d" % b, tag="z", bufs=Z_BANKS)
                 for g in range(PASSES):
-                    cols = slice((a * PASSES + g) * P, (a * PASSES + g + 1) * P)
+                    tokens = slice((a * PASSES + g) * P, (a * PASSES + g + 1) * P)
                     nc.tensor.matmul_mx(
-                        out=banks[k][:],
-                        lhsT=h_codes[i][:, cols].bitcast(FP8X4),
-                        lhsT_scale=h_blocks[i][:, cols],
+                        out=banks[b][:],
+                        lhsT=h_codes[i][:, tokens].bitcast(FP8X4),
+                        lhsT_scale=h_blocks[i][:, tokens],
                         rhs=w_codes[n, g][:].bitcast(FP8X4),
                         rhs_scale=w_blocks[n, g][:],
                         start=(g == 0),
                         stop=(g == PASSES - 1),
                     )
-                counts["multiplied"] = k + 1
+                counts["multiplied"] = b + 1
 
-        def drain(count=1):
-            for k in range(counts["drained"], counts["drained"] + count):
-                i, n, a = chunk(k)
+        def drain(count):
+            for b in range(counts["drained"], counts["drained"] + count):
+                i, n, a = bank_index(b)
                 if n == 0:
-                    t["nz", i, a] = row_tile(("zc", "zu")[a], i, ("neg_zc", "neg_zu")[a])
-                    if a == 0:
-                        stat("chunk_min", i, 2 * CHUNKS)
+                    neg_z[i, a] = buffer(z_tag(i, a), [P, V], F32, "neg_z%d_%d" % (i, a))
+                if n == 0 and a == 0:
+                    stat("chunk_min", i, BANKS_PER_TILE)
                 nc.vector.tensor_scalar(
-                    out=t["nz", i, a][:, n * BANK : (n + 1) * BANK], in0=banks[k][:], scalar1=-1.0, scalar2=None,
-                    op0=ALU.mult, op1=ALU.min, accum_out=t["chunk_min", i][:, a * CHUNKS + n : a * CHUNKS + n + 1],
+                    out=neg_z[i, a][:, n * BANK : (n + 1) * BANK], in0=banks[b][:], scalar1=-1.0, scalar2=None,
+                    op0=ALU.mult, op1=ALU.min, accum_out=stats["chunk_min", i][:, a * CHUNKS + n : a * CHUNKS + n + 1],
                 )
-                counts["drained"] = k + 1
+                counts["drained"] = b + 1
                 multiply_ahead()
 
         def row_max(i):
             nc.vector.tensor_reduce(
-                out=stat("neg_max", i, 2)[:], in_=t["chunk_min", i][:].rearrange("p (a n) -> p a n", a=2),
+                out=stat("neg_max", i, 2)[:], in_=stats["chunk_min", i][:].rearrange("p (a n) -> p a n", a=2),
                 axis=mybir.AxisListType.X, op=ALU.min,
             )
 
-        def max_gap(i):
-            neg_max = t["neg_max", i]
-            nc.vector.tensor_scalar(
-                out=stat("gap", i, 1)[:], in0=neg_max[:, 0:1], scalar1=neg_max[:, 1:2], scalar2=GUESS_TOP - 0.5,
-                op0=ALU.subtract, op1=ALU.add,
-            )
+        def subtract(i, engine, d_slot):
+            diff[i] = buffer("d%d" % d_slot, [P, V], F32, "diff%d" % i)
+            engine.tensor_tensor(out=diff[i][:], in0=neg_z[i, 1][:], in1=neg_z[i, 0][:], op=ALU.subtract)
 
         def exp(i, a):
             if a == 0:
                 stat("sums", i, 2)
-            t["e", i, a] = row_tile(("ec", "eu")[a], i, ("exp_c", "exp_u")[a])
+            exps[i, a] = buffer(e_tag(i, a), [P, V], F32, "exp%d_%d" % (i, a))
             nc.scalar.activation(
-                out=t["e", i, a][:], in_=t["nz", i, a][:], func=ACT.Exp, scale=-1.0,
-                bias=t["neg_max", i][:, a : a + 1], accum_out=t["sums", i][:, a : a + 1],
+                out=exps[i, a][:], in_=neg_z[i, a][:], func=ACT.Exp, scale=-1.0,
+                bias=stats["neg_max", i][:, a : a + 1], accum_out=stats["sums", i][:, a : a + 1],
             )
 
-        def difference(i, engine, slot):
-            t["d", i] = rows.tile([P, V], F32, name="d%d" % i, tag="d%d" % slot, align_bytes=64)
-            engine.tensor_tensor(out=t["d", i][:], in0=t["nz", i, 1][:], in1=t["nz", i, 0][:], op=ALU.subtract)
-
-        def inverse_sums(i):
-            nc.vector.reciprocal(out=stat("inv", i, 2)[:], in_=t["sums", i][:])
-
-        def ladder_count(i):
-            passed = stage.tile([P, STEPS], F32, name="passed%d" % i, tag="passed", bufs=1)
+        def guess(i):
+            sums, neg_max = stats["sums", i], stats["neg_max", i]
+            nc.vector.reciprocal(out=stat("inv", i, 2)[:], in_=sums[:])
+            nc.vector.tensor_scalar(
+                out=stat("gap", i, 1)[:], in0=neg_max[:, 0:1], scalar1=neg_max[:, 1:2], scalar2=GUESS_TOP - 0.5,
+                op0=ALU.subtract, op1=ALU.add,
+            )
+            below = stage.tile([P, STEPS], F32, name="below%d" % i, tag="below", bufs=1)
             nc.vector.scalar_tensor_tensor(
-                out=passed[:], in0=ladder[:], scalar=t["sums", i][:, 1:2], in1=t["sums", i][:, 0:1].to_broadcast([P, STEPS]),
+                out=below[:], in0=ladder[:], scalar=sums[:, 1:2], in1=sums[:, 0:1].to_broadcast([P, STEPS]),
                 op0=ALU.mult, op1=ALU.is_le, accum_out=stat("count", i, 1)[:],
             )
 
         def guess_terms(i):
-            nc.scalar.activation(out=stat("half_exp", i, 1)[:], in_=t["count", i][:], func=ACT.Exp, scale=-STEP, bias=GUESS_TOP - LN2)
-            nc.scalar.activation(out=stat("ratio", i, 1)[:], in_=t["sums", i][:, 0:1], func=ACT.Copy, scale=t["inv", i][:, 1:2])
-            nc.scalar.activation(out=stat("coarse", i, 1)[:], in_=t["count", i][:], func=ACT.Identity, scale=-STEP, bias=t["gap", i][:])
+            count = stats["count", i]
+            nc.scalar.activation(out=stat("half_exp", i, 1)[:], in_=count[:], func=ACT.Exp, scale=-STEP, bias=GUESS_TOP - LN2)
+            nc.scalar.activation(out=stat("ratio", i, 1)[:], in_=stats["sums", i][:, 0:1], func=ACT.Copy, scale=stats["inv", i][:, 1:2])
+            nc.scalar.activation(out=stat("coarse", i, 1)[:], in_=count[:], func=ACT.Identity, scale=-STEP, bias=stats["gap", i][:])
 
         def guess_square(i):
-            nc.scalar.activation(out=stat("fine", i, 1)[:], in_=t["half_exp", i][:], func=ACT.Square, scale=t["ratio", i][:], bias=-1.0)
-
-        def shift(i):
-            nc.scalar.activation(out=stat("shift", i, 1)[:], in_=t["coarse", i][:], func=ACT.Identity, scale=0.5, bias=t["fine", i][:])
-
-        def tanh(i):
-            t["u", i] = row_tile("zu", i, "u")
-            nc.scalar.activation(out=t["u", i][:], in_=t["d", i][:], func=ACT.Tanh, scale=0.5, bias=t["shift", i][:])
-
-        def log(i, a, part=0, parts=1):
-            cols = slice(part * V // parts, (part + 1) * V // parts)
-            if a == 0 and part == 0:
-                t["log", i, 0] = stage.tile([P, V], F32, name="log_plus%d" % i, tag="log_plus")
-                t["log", i, 1] = t["u", i]
-            nc.scalar.activation(out=t["log", i, a][:, cols], in_=t["u", i][:, cols], func=ACT.Ln, scale=(SHRINK, -SHRINK)[a], bias=1.0)
-
-        def kl(i, a, part=0, parts=1):
-            cols = slice(part * V // parts, (part + 1) * V // parts)
-            if a == 0 and part == 0:
-                stat("kl", i, 2 * parts)
-            nc.vector.scalar_tensor_tensor(
-                out=t["log", i, a][:, cols], in0=t["log", i, a][:, cols], scalar=t["inv", i][:, a : a + 1], in1=t["e", i, a][:, cols],
-                op0=ALU.mult, op1=ALU.mult, accum_out=t["kl", i][:, 2 * part + a : 2 * part + a + 1],
+            nc.scalar.activation(
+                out=stat("fine", i, 1)[:], in_=stats["half_exp", i][:], func=ACT.Square, scale=stats["ratio", i][:], bias=-1.0
             )
 
-        def weight(i):
+        def shift(i):
+            nc.scalar.activation(
+                out=stat("shift", i, 1)[:], in_=stats["coarse", i][:], func=ACT.Identity, scale=0.5, bias=stats["fine", i][:]
+            )
+
+        def tanh(i):
+            tanh_u[i] = buffer(z_tag(i, 1), [P, V], F32, "u%d" % i)
+            nc.scalar.activation(out=tanh_u[i][:], in_=diff[i][:], func=ACT.Tanh, scale=0.5, bias=stats["shift", i][:])
+
+        def columns(part, parts):
+            return slice(part * V // parts, (part + 1) * V // parts)
+
+        def log(i, a, part=0, parts=1):
+            if a == 0 and part == 0:
+                logs[i, 0] = stage.tile([P, V], F32, name="log_plus%d" % i, tag="log_plus")
+                logs[i, 1] = tanh_u[i]
+            cols = columns(part, parts)
+            nc.scalar.activation(out=logs[i, a][:, cols], in_=tanh_u[i][:, cols], func=ACT.Ln, scale=(SHRINK, -SHRINK)[a], bias=1.0)
+
+        def weigh(i, a, part=0, parts=1):
+            if a == 0 and part == 0:
+                stat("partial", i, 2 * parts)
+            cols = columns(part, parts)
+            nc.vector.scalar_tensor_tensor(
+                out=logs[i, a][:, cols], in0=logs[i, a][:, cols], scalar=stats["inv", i][:, a : a + 1], in1=exps[i, a][:, cols],
+                op0=ALU.mult, op1=ALU.mult, accum_out=stats["partial", i][:, 2 * part + a : 2 * part + a + 1],
+            )
+
+        def divergence(i):
+            partial = stats["partial", i]
             nc.vector.tensor_scalar(
-                out=t["kl", i][:], in0=t["kl", i][:], scalar1=0.5 / LN2, scalar2=None,
-                op0=ALU.mult, op1=ALU.add, accum_out=stat("a", i, 1)[:],
+                out=partial[:], in0=partial[:], scalar1=0.5 / LN2, scalar2=None,
+                op0=ALU.mult, op1=ALU.add, accum_out=stat("jsd", i, 1)[:],
             )
 
         def combine(i, parts=1):
-            result = row_tile("ec", i, "result")
-            for s in range(parts):
-                cols = slice(s * V // parts, (s + 1) * V // parts)
+            result = buffer(e_tag(i, 0), [P, V], F32, "result%d" % i)
+            for part in range(parts):
+                cols = columns(part, parts)
                 nc.vector.scalar_tensor_tensor(
-                    out=result[:, cols], in0=t["d", i][:, cols], scalar=t["a", i][:], in1=t["nz", i, 0][:, cols],
+                    out=result[:, cols], in0=diff[i][:, cols], scalar=stats["jsd", i][:], in1=neg_z[i, 0][:, cols],
                     op0=ALU.mult, op1=ALU.subtract,
                 )
                 nc.sync.dma_start(out=out[i * P : (i + 1) * P, cols], in_=result[:, cols])
 
-        def guess(i):
-            inverse_sums(i)
-            max_gap(i)
-            ladder_count(i)
+        def finish(i, parts=1):
+            weigh(i, 0)
+            weigh(i, 1)
+            divergence(i)
+            combine(i, parts)
 
-        nc.sync.dma_start(out=scale[:], in_=w_scale.rearrange("(g p t) o -> p g (t o)", p=P, t=PACK))
-        load_w(0)
-        load_w(1)
+        def drain_tile(i):
+            drain(BANKS_PER_TILE)
+            row_max(i)
+
+        nc.scalar.dma_start(out=scale[:], in_=w_scale.rearrange("(g p t) o -> p g (t o)", p=P, t=PACK))
+        for j in range(3):
+            load_w(j)
         load_h(0)
-        for j in range(2, len(pieces)):
+        for j in range(3, len(pieces)):
             load_w(j)
         load_h(1)
         make_identity(nc, identity[:])
         nc.gpsimd.iota(ladder[:], pattern=[[1, STEPS]], base=0, channel_multiplier=0, allow_small_or_imprecise_dtypes=True)
         nc.scalar.activation(out=ladder[:], in_=ladder[:], func=ACT.Exp, scale=STEP, bias=-LOG_SPAN)
         turn(0)
-        for j in range(6):
-            widen(j, 2 if j < 2 else 0)
+        for j in range(len(pieces) - 2):
+            widen(j, PACK // 2 if j < 2 else 0)
             if j == 2:
                 regroup(0, nc.scalar.copy)
                 turn(1)
@@ -285,152 +304,118 @@ def tile_adacadjsdcontrastlogits_kernel(tc, hc, hu, w_bytes, w_scale, out):
         drain(2)
         quantize_w(7)
         quantize_w(6)
-        regroup(2, nc.scalar.copy, 0)
+        regroup(2, nc.scalar.copy, d_slot=0)
         quantize_h(1)
         turn(3)
         drain(2)
         row_max(0)
         quantize_h(2)
-        difference(0, nc.gpsimd, 0)
-        exp(0, 0)
-        exp(0, 1)
-        regroup(3, nc.scalar.copy, 1)
-        drain(4)
-        turn(4)
-        drain(4)
-        row_max(1)
-        exp(1, 0)
-        guess(0)
-        quantize_h(3)
-        difference(1, nc.gpsimd, 1)
-        guess_terms(0)
-        exp(1, 1)
-        guess_square(0)
-        regroup(4, nc.scalar.copy, 2)
-        shift(0)
-        drain(8)
-        turn(5)
-        row_max(2)
-        tanh(0)
-        guess(1)
-        quantize_h(4)
-        difference(2, nc.gpsimd, 2)
-        exp(2, 0)
-        guess_terms(1)
-        exp(2, 1)
-        guess_square(1)
-        drain(4)
-        regroup(5, nc.vector.tensor_copy, 3)
-        drain(4)
-        shift(1)
-        tanh(1)
-        turn(6)
-        row_max(3)
-        guess(2)
-        quantize_h(5)
-        difference(3, nc.gpsimd, 3)
-        guess_terms(2)
-        guess_square(2)
-        shift(2)
-        tanh(2)
-        drain(4)
-        regroup(6, nc.vector.tensor_copy)
-        drain(4)
-        row_max(4)
-        turn(7)
+
+        for i in range(4):
+            subtract(i, nc.gpsimd, d_slot=i)
+            if i < 3:
+                exp(i, 0)
+            if i > 0:
+                guess_terms(i - 1)
+            if i < 3:
+                exp(i, 1)
+            if i > 0:
+                guess_square(i - 1)
+            if i < 2:
+                regroup(i + 3, nc.scalar.copy, d_slot=i + 1)
+            if i > 0:
+                shift(i - 1)
+                tanh(i - 1)
+            drain(CHUNKS)
+            if i >= 2:
+                regroup(i + 3, nc.vector.tensor_copy, d_slot=3 if i == 2 else None)
+            drain(CHUNKS)
+            turn(i + 4)
+            row_max(i + 1)
+            if i < 3:
+                guess(i)
+            quantize_h(i + 3)
+
         log(0, 0)
         log(0, 1)
-        quantize_h(6)
-        kl(0, 0)
-        kl(0, 1)
-        log(1, 0)
-        log(1, 1)
-        log(2, 0)
-        log(2, 1)
-        kl(1, 0)
-        weight(0)
-        kl(1, 1)
+        weigh(0, 0)
+        weigh(0, 1)
+        for i in (1, 2):
+            log(i, 0)
+            log(i, 1)
+        weigh(1, 0)
+        divergence(0)
+        weigh(1, 1)
         combine(0)
-        weight(1)
-        regroup(7, nc.vector.tensor_copy, 0)
+        divergence(1)
+        regroup(7, nc.vector.tensor_copy, d_slot=0)
         combine(1)
-        difference(4, nc.gpsimd, 1)
-        drain(8)
-        row_max(5)
-        exp(3, 0)
-        exp(3, 1)
-        exp(4, 0)
-        exp(4, 1)
+
+        subtract(4, nc.gpsimd, d_slot=1)
+        drain_tile(5)
+        for i in (3, 4):
+            exp(i, 0)
+            exp(i, 1)
         exp(5, 0)
         guess(3)
         guess(4)
         quantize_h(7)
-        difference(5, nc.gpsimd, 0)
-        drain(8)
-        row_max(6)
+        subtract(5, nc.gpsimd, d_slot=0)
+        drain_tile(6)
         guess_terms(3)
         guess_terms(4)
         exp(5, 1)
-        guess_square(3)
-        guess_square(4)
-        shift(3)
-        shift(4)
+        for step in (guess_square, shift):
+            step(3)
+            step(4)
         tanh(3)
         guess(5)
-        kl(2, 0)
-        kl(2, 1)
         guess_terms(5)
         tanh(4)
         guess_square(5)
         shift(5)
         tanh(5)
-        weight(2)
-        combine(2)
-        difference(6, nc.gpsimd, 2)
-        drain(8)
-        row_max(7)
+        finish(2)
+        subtract(6, nc.gpsimd, d_slot=2)
+        drain_tile(7)
+
         log(3, 0)
         log(3, 1)
-        kl(3, 0)
-        kl(3, 1)
-        log(4, 0)
-        log(4, 1)
-        log(5, 0)
-        log(5, 1)
-        weight(3)
-        combine(3)
-        kl(4, 0)
-        kl(4, 1)
-        difference(7, nc.vector, 3)
-        weight(4)
+        finish(3)
+        for i in (4, 5):
+            log(i, 0)
+            log(i, 1)
+        weigh(4, 0)
+        weigh(4, 1)
+        subtract(7, nc.vector, d_slot=3)
+        divergence(4)
+
         exp(6, 0)
         exp(6, 1)
         guess(6)
         combine(4)
-        kl(5, 0)
+        weigh(5, 0)
         exp(7, 0)
         guess_terms(6)
         exp(7, 1)
         guess_square(6)
         shift(6)
         guess(7)
-        kl(5, 1)
+        weigh(5, 1)
         tanh(6)
         guess_terms(7)
         guess_square(7)
         shift(7)
         tanh(7)
-        weight(5)
+        divergence(5)
         combine(5)
+
         for part in range(2):
             for a in range(2):
                 log(6, a, part, 2)
-                kl(6, a, part, 2)
+                weigh(6, a, part, 2)
         log(7, 0)
         log(7, 1)
-        weight(6)
-        combine(6, 2)
-        kl(7, 0)
-        kl(7, 1)
-        weight(7)
-        combine(7, 4)
+        divergence(6)
+        combine(6, parts=2)
+        finish(7, parts=4)

@@ -220,12 +220,17 @@ def tile_adacadjsdcontrastlogits_kernel(tc, hc, hu, w_bytes, w_scale, out):
                 out=stat("shift", i, 1)[:], in_=stats["coarse", i][:], func=ACT.Identity, scale=0.5, bias=stats["fine", i][:]
             )
 
-        def tanh(i):
-            tanh_u[i] = buffer(z_tag(i, 1), [P, V], F32, "u%d" % i)
-            nc.scalar.activation(out=tanh_u[i][:], in_=diff[i][:], func=ACT.Tanh, scale=0.5, bias=stats["shift", i][:])
-
         def columns(part, parts):
             return slice(part * V // parts, (part + 1) * V // parts)
+
+        def tanh(i, then_shift=None):
+            tanh_u[i] = buffer(z_tag(i, 1), [P, V], F32, "u%d" % i)
+            between = [] if then_shift is None else [guess_terms, guess_square, shift]
+            for part in range(len(between) + 1):
+                cols = columns(part, len(between) + 1)
+                nc.scalar.activation(out=tanh_u[i][:, cols], in_=diff[i][:, cols], func=ACT.Tanh, scale=0.5, bias=stats["shift", i][:])
+                if part < len(between):
+                    between[part](then_shift)
 
         def log(i, a, part=0, parts=1):
             if a == 0 and part == 0:
@@ -311,30 +316,35 @@ def tile_adacadjsdcontrastlogits_kernel(tc, hc, hu, w_bytes, w_scale, out):
         row_max(0)
         quantize_h(2)
 
-        for i in range(4):
+        for i in range(3):
             subtract(i, nc.gpsimd, d_slot=i)
-            if i < 3:
-                exp(i, 0)
+            exp(i, 0)
             if i > 0:
                 guess_terms(i - 1)
-            if i < 3:
-                exp(i, 1)
+            exp(i, 1)
             if i > 0:
                 guess_square(i - 1)
             if i < 2:
                 regroup(i + 3, nc.scalar.copy, d_slot=i + 1)
             if i > 0:
                 shift(i - 1)
-                tanh(i - 1)
-            drain(CHUNKS)
-            if i >= 2:
-                regroup(i + 3, nc.vector.tensor_copy, d_slot=3 if i == 2 else None)
-            drain(CHUNKS)
+            if i == 1:
+                tanh(0)
+            drain_tile(i + 1)
+            guess(i)
+            if i == 2:
+                regroup(i + 3, nc.vector.tensor_copy, d_slot=i + 1)
             turn(i + 4)
-            row_max(i + 1)
-            if i < 3:
-                guess(i)
             quantize_h(i + 3)
+        subtract(3, nc.gpsimd, d_slot=3)
+        tanh(1, then_shift=2)
+        tanh(2)
+        drain(CHUNKS)
+        regroup(6, nc.vector.tensor_copy)
+        drain(CHUNKS)
+        turn(7)
+        row_max(4)
+        quantize_h(6)
 
         log(0, 0)
         log(0, 1)
@@ -363,17 +373,12 @@ def tile_adacadjsdcontrastlogits_kernel(tc, hc, hu, w_bytes, w_scale, out):
         subtract(5, nc.gpsimd, d_slot=0)
         drain_tile(6)
         guess_terms(3)
-        guess_terms(4)
         exp(5, 1)
-        for step in (guess_square, shift):
-            step(3)
-            step(4)
-        tanh(3)
+        guess_square(3)
+        shift(3)
+        tanh(3, then_shift=4)
         guess(5)
-        guess_terms(5)
-        tanh(4)
-        guess_square(5)
-        shift(5)
+        tanh(4, then_shift=5)
         tanh(5)
         finish(2)
         subtract(6, nc.gpsimd, d_slot=2)
@@ -402,10 +407,7 @@ def tile_adacadjsdcontrastlogits_kernel(tc, hc, hu, w_bytes, w_scale, out):
         shift(6)
         guess(7)
         weigh(5, 1)
-        tanh(6)
-        guess_terms(7)
-        guess_square(7)
-        shift(7)
+        tanh(6, then_shift=7)
         tanh(7)
         divergence(5)
         combine(5)

@@ -27,6 +27,8 @@ Z_BANKS = 6
 Z_SLOTS = 5
 E_SLOTS = 4
 
+SPACER = 384
+
 LN2 = math.log(2.0)
 SHRINK = 1.0 - 2.0**-24
 STEPS = 256
@@ -64,6 +66,9 @@ def tile_adacadjsdcontrastlogits_kernel(tc, hc, hu, w_bytes, w_scale, out):
             stats[name, i] = keep.tile([P, width], F32, name="%s%d" % (name, i))
             return stats[name, i]
 
+        def columns(part, parts):
+            return slice(part * V // parts, (part + 1) * V // parts)
+
         scale = keep.tile([P, PASSES, PACK], F32, name="scale")
         identity = keep.tile([P, P], F32, name="identity")
         ladder = keep.tile([P, STEPS], F32, name="ladder")
@@ -85,7 +90,8 @@ def tile_adacadjsdcontrastlogits_kernel(tc, hc, hu, w_bytes, w_scale, out):
                     nc.scalar.activation(out=w_planes[j][:, t, :], in_=codes, func=ACT.Copy, scale=factor)
 
         def interleave(j, copy):
-            w_grouped[j] = buffer(e_tag(2, j % 2), [P, BANK, PACK], BF16, "w_grouped%d" % j)
+            tag = (e_tag(2, 0), e_tag(2, 1), e_tag(1, 1))[j % 3]
+            w_grouped[j] = buffer(tag, [P, BANK, PACK], BF16, "w_grouped%d" % j)
             copy(
                 out=w_grouped[j][:].rearrange("p (c x) t -> p c t x", x=4),
                 in_=w_planes[j][:].rearrange("p t (c x) -> p c t x", x=4),
@@ -178,26 +184,40 @@ def tile_adacadjsdcontrastlogits_kernel(tc, hc, hu, w_bytes, w_scale, out):
                 axis=mybir.AxisListType.X, op=ALU.min,
             )
 
+        def subtract_part(i, engine, cols):
+            engine.tensor_tensor(out=diff[i][:, cols], in0=neg_z[i, 1][:, cols], in1=neg_z[i, 0][:, cols], op=ALU.subtract)
+
         def subtract(i, engine, d_slot):
             diff[i] = buffer("d%d" % d_slot, [P, V], F32, "diff%d" % i)
-            engine.tensor_tensor(out=diff[i][:], in0=neg_z[i, 1][:], in1=neg_z[i, 0][:], op=ALU.subtract)
+            subtract_part(i, engine, columns(0, 1))
 
-        def exp(i, a):
-            if a == 0:
-                stat("sums", i, 2)
-            exps[i, a] = buffer(e_tag(i, a), [P, V], F32, "exp%d_%d" % (i, a))
-            nc.scalar.activation(
-                out=exps[i, a][:], in_=neg_z[i, a][:], func=ACT.Exp, scale=-1.0,
-                bias=stats["neg_max", i][:, a : a + 1], accum_out=stats["sums", i][:, a : a + 1],
-            )
+        def exp(i, then_shift=None):
+            between = [] if then_shift is None else [guess_terms, guess_square, shift]
+            parts = 2 if between else 1
+            sums = stat("half_sums" if between else "sums", i, 2 * parts)
+            for a in range(2):
+                exps[i, a] = buffer(e_tag(i, a), [P, V], F32, "exp%d_%d" % (i, a))
+                for part in range(parts):
+                    cols, k = columns(part, parts), a * parts + part
+                    nc.scalar.activation(
+                        out=exps[i, a][:, cols], in_=neg_z[i, a][:, cols], func=ACT.Exp, scale=-1.0,
+                        bias=stats["neg_max", i][:, a : a + 1], accum_out=sums[:, k : k + 1],
+                    )
+                    if k < len(between):
+                        between[k](then_shift)
 
         def guess(i):
+            if ("half_sums", i) in stats:
+                nc.vector.tensor_reduce(
+                    out=stat("sums", i, 2)[:], in_=stats["half_sums", i][:].rearrange("p (a h) -> p a h", a=2),
+                    axis=mybir.AxisListType.X, op=ALU.add,
+                )
             sums, neg_max = stats["sums", i], stats["neg_max", i]
-            nc.vector.reciprocal(out=stat("inv", i, 2)[:], in_=sums[:])
             nc.vector.tensor_scalar(
                 out=stat("gap", i, 1)[:], in0=neg_max[:, 0:1], scalar1=neg_max[:, 1:2], scalar2=GUESS_TOP - 0.5,
                 op0=ALU.subtract, op1=ALU.add,
             )
+            nc.vector.reciprocal(out=stat("inv", i, 2)[:], in_=sums[:])
             below = stage.tile([P, STEPS], F32, name="below%d" % i, tag="below", bufs=1)
             nc.vector.scalar_tensor_tensor(
                 out=below[:], in0=ladder[:], scalar=sums[:, 1:2], in1=sums[:, 0:1].to_broadcast([P, STEPS]),
@@ -220,24 +240,25 @@ def tile_adacadjsdcontrastlogits_kernel(tc, hc, hu, w_bytes, w_scale, out):
                 out=stat("shift", i, 1)[:], in_=stats["coarse", i][:], func=ACT.Identity, scale=0.5, bias=stats["fine", i][:]
             )
 
-        def columns(part, parts):
-            return slice(part * V // parts, (part + 1) * V // parts)
-
         def tanh(i, then_shift=None):
             tanh_u[i] = buffer(z_tag(i, 1), [P, V], F32, "u%d" % i)
             between = [] if then_shift is None else [guess_terms, guess_square, shift]
-            for part in range(len(between) + 1):
-                cols = columns(part, len(between) + 1)
+            edges = [0] + [V - SPACER * (len(between) - k) for k in range(len(between) + 1)]
+            for k in range(len(between) + 1):
+                cols = slice(edges[k], edges[k + 1])
                 nc.scalar.activation(out=tanh_u[i][:, cols], in_=diff[i][:, cols], func=ACT.Tanh, scale=0.5, bias=stats["shift", i][:])
-                if part < len(between):
-                    between[part](then_shift)
+                if k < len(between):
+                    between[k](then_shift)
 
-        def log(i, a, part=0, parts=1):
-            if a == 0 and part == 0:
-                logs[i, 0] = stage.tile([P, V], F32, name="log_plus%d" % i, tag="log_plus")
-                logs[i, 1] = tanh_u[i]
-            cols = columns(part, parts)
-            nc.scalar.activation(out=logs[i, a][:, cols], in_=tanh_u[i][:, cols], func=ACT.Ln, scale=(SHRINK, -SHRINK)[a], bias=1.0)
+        def log(i):
+            logs[i, 0] = stage.tile([P, V], F32, name="log_plus%d" % i, tag="log_plus")
+            logs[i, 1] = tanh_u[i]
+            for a in range(2):
+                for half in range(2):
+                    cols = columns(half, 2)
+                    nc.scalar.activation(
+                        out=logs[i, a][:, cols], in_=tanh_u[i][:, cols], func=ACT.Ln, scale=(SHRINK, -SHRINK)[a], bias=1.0
+                    )
 
         def weigh(i, a, part=0, parts=1):
             if a == 0 and part == 0:
@@ -255,7 +276,7 @@ def tile_adacadjsdcontrastlogits_kernel(tc, hc, hu, w_bytes, w_scale, out):
                 op0=ALU.mult, op1=ALU.add, accum_out=stat("jsd", i, 1)[:],
             )
 
-        def combine(i, parts=1):
+        def combine(i, parts=2):
             result = buffer(e_tag(i, 0), [P, V], F32, "result%d" % i)
             for part in range(parts):
                 cols = columns(part, parts)
@@ -265,11 +286,11 @@ def tile_adacadjsdcontrastlogits_kernel(tc, hc, hu, w_bytes, w_scale, out):
                 )
                 nc.sync.dma_start(out=out[i * P : (i + 1) * P, cols], in_=result[:, cols])
 
-        def finish(i, parts=1):
+        def finish(i):
             weigh(i, 0)
             weigh(i, 1)
             divergence(i)
-            combine(i, parts)
+            combine(i)
 
         def drain_tile(i):
             drain(BANKS_PER_TILE)
@@ -286,8 +307,11 @@ def tile_adacadjsdcontrastlogits_kernel(tc, hc, hu, w_bytes, w_scale, out):
         nc.gpsimd.iota(ladder[:], pattern=[[1, STEPS]], base=0, channel_multiplier=0, allow_small_or_imprecise_dtypes=True)
         nc.scalar.activation(out=ladder[:], in_=ladder[:], func=ACT.Exp, scale=STEP, bias=-LOG_SPAN)
         turn(0)
+        widen(0, on_vector=PACK // 2)
+        widen(1, on_vector=PACK // 2)
         for j in range(len(pieces) - 2):
-            widen(j, PACK // 2 if j < 2 else 0)
+            if j >= 2:
+                widen(j, on_vector=PACK // 2 if j == 2 else 0)
             if j == 2:
                 regroup(0, nc.scalar.copy)
                 turn(1)
@@ -316,27 +340,25 @@ def tile_adacadjsdcontrastlogits_kernel(tc, hc, hu, w_bytes, w_scale, out):
         row_max(0)
         quantize_h(2)
 
-        for i in range(3):
-            subtract(i, nc.gpsimd, d_slot=i)
-            exp(i, 0)
-            if i > 0:
-                guess_terms(i - 1)
-            exp(i, 1)
-            if i > 0:
-                guess_square(i - 1)
-            if i < 2:
-                regroup(i + 3, nc.scalar.copy, d_slot=i + 1)
-            if i > 0:
-                shift(i - 1)
-            if i == 1:
-                tanh(0)
+        def drain_round(i):
             drain_tile(i + 1)
             guess(i)
             if i == 2:
                 regroup(i + 3, nc.vector.tensor_copy, d_slot=i + 1)
             turn(i + 4)
             quantize_h(i + 3)
-        subtract(3, nc.gpsimd, d_slot=3)
+            subtract(i + 1, nc.gpsimd, d_slot=i + 1)
+
+        subtract(0, nc.gpsimd, d_slot=0)
+        exp(0)
+        regroup(3, nc.scalar.copy, d_slot=1)
+        drain_round(0)
+        exp(1, then_shift=0)
+        regroup(4, nc.scalar.copy, d_slot=2)
+        drain_round(1)
+        tanh(0, then_shift=1)
+        exp(2)
+        drain_round(2)
         tanh(1, then_shift=2)
         tanh(2)
         drain(CHUNKS)
@@ -346,13 +368,11 @@ def tile_adacadjsdcontrastlogits_kernel(tc, hc, hu, w_bytes, w_scale, out):
         row_max(4)
         quantize_h(6)
 
-        log(0, 0)
-        log(0, 1)
+        log(0)
         weigh(0, 0)
         weigh(0, 1)
-        for i in (1, 2):
-            log(i, 0)
-            log(i, 1)
+        log(1)
+        log(2)
         weigh(1, 0)
         divergence(0)
         weigh(1, 1)
@@ -363,19 +383,14 @@ def tile_adacadjsdcontrastlogits_kernel(tc, hc, hu, w_bytes, w_scale, out):
 
         subtract(4, nc.gpsimd, d_slot=1)
         drain_tile(5)
-        for i in (3, 4):
-            exp(i, 0)
-            exp(i, 1)
-        exp(5, 0)
+        exp(3)
+        exp(4)
         guess(3)
         guess(4)
         quantize_h(7)
         subtract(5, nc.gpsimd, d_slot=0)
         drain_tile(6)
-        guess_terms(3)
-        exp(5, 1)
-        guess_square(3)
-        shift(3)
+        exp(5, then_shift=3)
         tanh(3, then_shift=4)
         guess(5)
         tanh(4, then_shift=5)
@@ -384,40 +399,41 @@ def tile_adacadjsdcontrastlogits_kernel(tc, hc, hu, w_bytes, w_scale, out):
         subtract(6, nc.gpsimd, d_slot=2)
         drain_tile(7)
 
-        log(3, 0)
-        log(3, 1)
+        log(3)
         finish(3)
-        for i in (4, 5):
-            log(i, 0)
-            log(i, 1)
+        log(4)
+        log(5)
         weigh(4, 0)
         weigh(4, 1)
-        subtract(7, nc.vector, d_slot=3)
-        divergence(4)
 
-        exp(6, 0)
-        exp(6, 1)
+        exp(6)
+        diff[7] = buffer("d3", [P, V], F32, "diff7")
+        subtract_part(7, nc.vector, columns(0, 2))
+        divergence(4)
         guess(6)
+        subtract_part(7, nc.vector, columns(1, 2))
         combine(4)
-        weigh(5, 0)
-        exp(7, 0)
-        guess_terms(6)
-        exp(7, 1)
-        guess_square(6)
-        shift(6)
+        weigh(5, 0, 0, 2)
+        exp(7, then_shift=6)
         guess(7)
-        weigh(5, 1)
+        weigh(5, 0, 1, 2)
+        weigh(5, 1, 0, 2)
+        weigh(5, 1, 1, 2)
         tanh(6, then_shift=7)
         tanh(7)
         divergence(5)
         combine(5)
 
-        for part in range(2):
-            for a in range(2):
-                log(6, a, part, 2)
-                weigh(6, a, part, 2)
-        log(7, 0)
-        log(7, 1)
+        log(6)
+        log(7)
+        for a in range(2):
+            for half in range(2):
+                weigh(6, a, half, 2)
+        weigh(7, 0, 0, 2)
         divergence(6)
-        combine(6, parts=2)
-        finish(7, parts=4)
+        weigh(7, 0, 1, 2)
+        combine(6)
+        weigh(7, 1, 0, 2)
+        weigh(7, 1, 1, 2)
+        divergence(7)
+        combine(7, parts=4)

import math
from contextlib import ExitStack

import concourse.mybir as mybir
from concourse.masks import make_identity

N, D, V = 1024, 1024, 2048
FLOPS = 2 * 2 * N * D * V

F32 = mybir.dt.float32
BF16 = mybir.dt.bfloat16
U32 = mybir.dt.uint32
U8 = mybir.dt.uint8
FP8 = mybir.dt.float8_e4m3fn
FP8X4 = mybir.dt.float8_e4m3fn_x4
ALU = mybir.AluOpType
ACT = mybir.ActivationFunctionType

P = 128
PACK = 4
PASSES = D // (P * PACK)
BANK = 512
CHUNKS = V // BANK
TILES = N // P
BANKS_PER_TILE = 2 * CHUNKS
Z_BANKS = 6
Z_SLOTS = 5
E_SLOTS = 4

SPACER = 384

LN2 = math.log(2.0)
SHRINK = 1.0 - 2.0**-24
STEPS = 256
LOG_SPAN = math.log(V)
STEP = 2.0 * LOG_SPAN / STEPS
GUESS_TOP = LOG_SPAN + STEP / 2.0


def tile_adacadjsdcontrastlogits_kernel(tc, hc, hu, w_bytes, w_scale, out):
    nc = tc.nc
    with ExitStack() as ctx:
        keep = ctx.enter_context(tc.tile_pool(name="keep", bufs=1))
        rows = ctx.enter_context(tc.tile_pool(name="rows", bufs=1))
        stage = ctx.enter_context(tc.tile_pool(name="stage", bufs=2))
        psum = ctx.enter_context(tc.psum_pool(name="psum", bufs=1))
        ctx.enter_context(tc.manual_schedule())

        pieces = [(n, g) for n in range(CHUNKS) for g in range(PASSES)]
        w_view = w_bytes.rearrange("(g p t) n -> g p t n", p=P, t=PACK)
        w_raw, w_planes, w_grouped, w_codes, w_blocks = {}, {}, {}, {}, {}
        h_raw, h_turned, h_grouped, h_codes, h_blocks = {}, {}, {}, {}, {}
        banks, neg_z, exps, diff, tanh_u, logs, stats = {}, {}, {}, {}, {}, {}, {}
        counts = {"multiplied": 0, "drained": 0}

        def buffer(tag, shape, dtype, name):
            return rows.tile(shape, dtype, name=name, tag=tag, align_bytes=64)

        def z_tag(i, a):
            return "z%d_%d" % (a, i % Z_SLOTS)

        def e_tag(i, a):
            return "e%d_%d" % (a, i % E_SLOTS)

        def stat(name, i, width):
            stats[name, i] = keep.tile([P, width], F32, name="%s%d" % (name, i))
            return stats[name, i]

        def columns(part, parts):
            return slice(part * V // parts, (part + 1) * V // parts)

        scale = keep.tile([P, PASSES, PACK], F32, name="scale")
        identity = keep.tile([P, P], F32, name="identity")
        ladder = keep.tile([P, STEPS], F32, name="ladder")

        def load_w(j):
            n, g = pieces[j]
            w_raw[j] = buffer(z_tag(1 + j // 2, j % 2), [P, PACK, BANK], U8, "w_raw%d" % j)
            nc.sync.dma_start(out=w_raw[j][:], in_=w_view[g][:, :, n * BANK : (n + 1) * BANK])

        def widen(j, on_vector=0):
            g = pieces[j][1]
            tag = (e_tag(3, 0), e_tag(3, 1), e_tag(1, 0))[j % 3]
            w_planes[j] = buffer(tag, [P, PACK, BANK], BF16, "w_planes%d" % j)
            for t in range(PACK):
                codes, factor = w_raw[j][:, t, :].bitcast(FP8), scale[:, g, t : t + 1]
                if t < on_vector:
                    nc.vector.tensor_scalar(out=w_planes[j][:, t, :], in0=codes, scalar1=factor, scalar2=None, op0=ALU.mult)
                else:
                    nc.scalar.activation(out=w_planes[j][:, t, :], in_=codes, func=ACT.Copy, scale=factor)

        def interleave(j, copy):
            tag = (e_tag(2, 0), e_tag(2, 1), e_tag(1, 1))[j % 3]
            w_grouped[j] = buffer(tag, [P, BANK, PACK], BF16, "w_grouped%d" % j)
            copy(
                out=w_grouped[j][:].rearrange("p (c x) t -> p c t x", x=4),
                in_=w_planes[j][:].rearrange("p t (c x) -> p c t x", x=4),
            )

        def quantize_w(j):
            w_codes[pieces[j]] = keep.tile([P, BANK], U32, name="w_codes%d" % j, align_bytes=64)
            w_blocks[pieces[j]] = keep.tile([P, BANK], U8, name="w_blocks%d" % j, align_bytes=64)
            nc.vector.quantize_mx(
                out=w_codes[pieces[j]][:].bitcast(FP8X4),
                scales=w_blocks[pieces[j]][:],
                in_=w_grouped[j][:].rearrange("p c t -> p (c t)"),
            )
            multiply_ahead()

        def load_h(i):
            for a, h in enumerate((hc, hu)):
                h_raw[i, a] = stage.tile([P, D], BF16, name="h_raw%d_%d" % (i, a), tag="h_raw%d" % a)
                nc.sync.dma_start(out=h_raw[i, a][:], in_=h[i * P : (i + 1) * P, :])

        def turn(i):
            for a in range(2):
                words = h_raw[i, a][:].bitcast(F32)
                h_turned[a] = psum.tile([P, PASSES, 2, P], F32, name="h_turned%d_%d" % (i, a), tag="h_turned%d" % a)
                for g in range(PASSES):
                    for v in range(2):
                        nc.tensor.transpose(h_turned[a][:, g, v, :], words[:, 256 * g + v : 256 * (g + 1) : 2], identity[:])
            if i + 2 < TILES:
                load_h(i + 2)

        def regroup(i, copy, d_slot=None):
            shape, name = [P, 2, PASSES, P, 2], "h_grouped%d" % i
            if d_slot is None:
                h_grouped[i] = stage.tile(shape, F32, name=name, tag="h_grouped", bufs=1, align_bytes=64)
            else:
                h_grouped[i] = buffer("d%d" % d_slot, shape, F32, name)
            for a in range(2):
                copy(out=h_grouped[i][:, a], in_=h_turned[a][:].rearrange("p g v r -> p g r v"))

        def quantize_h(i):
            h_codes[i] = stage.tile([P, 2 * PASSES * P], U32, name="h_codes%d" % i, tag="h_codes", bufs=3, align_bytes=64)
            h_blocks[i] = stage.tile([P, 2 * PASSES * P], U8, name="h_blocks%d" % i, tag="h_blocks", bufs=3, align_bytes=64)
            nc.vector.quantize_mx(
                out=h_codes[i][:].bitcast(FP8X4),
                scales=h_blocks[i][:],
                in_=h_grouped[i][:].rearrange("p a g r v -> p (a g r v)").bitcast(BF16),
            )
            multiply_ahead()

        def bank_index(b):
            return b // BANKS_PER_TILE, b % BANKS_PER_TILE // 2, b % 2

        def multiply_ahead():
            while counts["multiplied"] < min(counts["drained"] + Z_BANKS, TILES * BANKS_PER_TILE):
                b = counts["multiplied"]
                i, n, a = bank_index(b)
                if i not in h_codes or any((n, g) not in w_codes for g in range(PASSES)):
                    return
                banks[b] = psum.tile([P, BANK], F32, name="z%d" % b, tag="z", bufs=Z_BANKS)
                for g in range(PASSES):
                    tokens = slice((a * PASSES + g) * P, (a * PASSES + g + 1) * P)
                    nc.tensor.matmul_mx(
                        out=banks[b][:],
                        lhsT=h_codes[i][:, tokens].bitcast(FP8X4),
                        lhsT_scale=h_blocks[i][:, tokens],
                        rhs=w_codes[n, g][:].bitcast(FP8X4),
                        rhs_scale=w_blocks[n, g][:],
                        start=(g == 0),
                        stop=(g == PASSES - 1),
                    )
                counts["multiplied"] = b + 1

        def drain(count):
            for b in range(counts["drained"], counts["drained"] + count):
                i, n, a = bank_index(b)
                if n == 0:
                    neg_z[i, a] = buffer(z_tag(i, a), [P, V], F32, "neg_z%d_%d" % (i, a))
                if n == 0 and a == 0:
                    stat("chunk_min", i, BANKS_PER_TILE)
                nc.vector.tensor_scalar(
                    out=neg_z[i, a][:, n * BANK : (n + 1) * BANK], in0=banks[b][:], scalar1=-1.0, scalar2=None,
                    op0=ALU.mult, op1=ALU.min, accum_out=stats["chunk_min", i][:, a * CHUNKS + n : a * CHUNKS + n + 1],
                )
                counts["drained"] = b + 1
                multiply_ahead()

        def row_max(i):
            nc.vector.tensor_reduce(
                out=stat("neg_max", i, 2)[:], in_=stats["chunk_min", i][:].rearrange("p (a n) -> p a n", a=2),
                axis=mybir.AxisListType.X, op=ALU.min,
            )

        def subtract_part(i, engine, cols):
            engine.tensor_tensor(out=diff[i][:, cols], in0=neg_z[i, 1][:, cols], in1=neg_z[i, 0][:, cols], op=ALU.subtract)

        def subtract(i, engine, d_slot):
            diff[i] = buffer("d%d" % d_slot, [P, V], F32, "diff%d" % i)
            subtract_part(i, engine, columns(0, 1))

        def exp(i, then_shift=None):
            between = [] if then_shift is None else [guess_terms, guess_square, shift]
            parts = 2 if between else 1
            sums = stat("half_sums" if between else "sums", i, 2 * parts)
            for a in range(2):
                exps[i, a] = buffer(e_tag(i, a), [P, V], F32, "exp%d_%d" % (i, a))
                for part in range(parts):
                    cols, k = columns(part, parts), a * parts + part
                    nc.scalar.activation(
                        out=exps[i, a][:, cols], in_=neg_z[i, a][:, cols], func=ACT.Exp, scale=-1.0,
                        bias=stats["neg_max", i][:, a : a + 1], accum_out=sums[:, k : k + 1],
                    )
                    if k < len(between):
                        between[k](then_shift)

        def guess(i):
            if ("half_sums", i) in stats:
                nc.vector.tensor_reduce(
                    out=stat("sums", i, 2)[:], in_=stats["half_sums", i][:].rearrange("p (a h) -> p a h", a=2),
                    axis=mybir.AxisListType.X, op=ALU.add,
                )
            sums, neg_max = stats["sums", i], stats["neg_max", i]
            nc.vector.tensor_scalar(
                out=stat("gap", i, 1)[:], in0=neg_max[:, 0:1], scalar1=neg_max[:, 1:2], scalar2=GUESS_TOP - 0.5,
                op0=ALU.subtract, op1=ALU.add,
            )
            nc.vector.reciprocal(out=stat("inv", i, 2)[:], in_=sums[:])
            below = stage.tile([P, STEPS], F32, name="below%d" % i, tag="below", bufs=1)
            nc.vector.scalar_tensor_tensor(
                out=below[:], in0=ladder[:], scalar=sums[:, 1:2], in1=sums[:, 0:1].to_broadcast([P, STEPS]),
                op0=ALU.mult, op1=ALU.is_le, accum_out=stat("count", i, 1)[:],
            )

        def guess_terms(i):
            count = stats["count", i]
            nc.scalar.activation(out=stat("half_exp", i, 1)[:], in_=count[:], func=ACT.Exp, scale=-STEP, bias=GUESS_TOP - LN2)
            nc.scalar.activation(out=stat("ratio", i, 1)[:], in_=stats["sums", i][:, 0:1], func=ACT.Copy, scale=stats["inv", i][:, 1:2])
            nc.scalar.activation(out=stat("coarse", i, 1)[:], in_=count[:], func=ACT.Identity, scale=-STEP, bias=stats["gap", i][:])

        def guess_square(i):
            nc.scalar.activation(
                out=stat("fine", i, 1)[:], in_=stats["half_exp", i][:], func=ACT.Square, scale=stats["ratio", i][:], bias=-1.0
            )

        def shift(i):
            nc.scalar.activation(
                out=stat("shift", i, 1)[:], in_=stats["coarse", i][:], func=ACT.Identity, scale=0.5, bias=stats["fine", i][:]
            )

        def tanh(i, then_shift=None):
            tanh_u[i] = buffer(z_tag(i, 1), [P, V], F32, "u%d" % i)
            between = [] if then_shift is None else [guess_terms, guess_square, shift]
            edges = [0] + [V - SPACER * (len(between) - k) for k in range(len(between) + 1)]
            for k in range(len(between) + 1):
                cols = slice(edges[k], edges[k + 1])
                nc.scalar.activation(out=tanh_u[i][:, cols], in_=diff[i][:, cols], func=ACT.Tanh, scale=0.5, bias=stats["shift", i][:])
                if k < len(between):
                    between[k](then_shift)

        def log(i):
            logs[i, 0] = stage.tile([P, V], F32, name="log_plus%d" % i, tag="log_plus")
            logs[i, 1] = tanh_u[i]
            for a in range(2):
                for half in range(2):
                    cols = columns(half, 2)
                    nc.scalar.activation(
                        out=logs[i, a][:, cols], in_=tanh_u[i][:, cols], func=ACT.Ln, scale=(SHRINK, -SHRINK)[a], bias=1.0
                    )

        def weigh(i, a, part=0, parts=1):
            if a == 0 and part == 0:
                stat("partial", i, 2 * parts)
            cols = columns(part, parts)
            nc.vector.scalar_tensor_tensor(
                out=logs[i, a][:, cols], in0=logs[i, a][:, cols], scalar=stats["inv", i][:, a : a + 1], in1=exps[i, a][:, cols],
                op0=ALU.mult, op1=ALU.mult, accum_out=stats["partial", i][:, 2 * part + a : 2 * part + a + 1],
            )

        def divergence(i):
            partial = stats["partial", i]
            nc.vector.tensor_scalar(
                out=partial[:], in0=partial[:], scalar1=0.5 / LN2, scalar2=None,
                op0=ALU.mult, op1=ALU.add, accum_out=stat("jsd", i, 1)[:],
            )

        def combine(i, parts=2):
            result = buffer(e_tag(i, 0), [P, V], F32, "result%d" % i)
            for part in range(parts):
                cols = columns(part, parts)
                nc.vector.scalar_tensor_tensor(
                    out=result[:, cols], in0=diff[i][:, cols], scalar=stats["jsd", i][:], in1=neg_z[i, 0][:, cols],
                    op0=ALU.mult, op1=ALU.subtract,
                )
                nc.sync.dma_start(out=out[i * P : (i + 1) * P, cols], in_=result[:, cols])

        def finish(i):
            weigh(i, 0)
            weigh(i, 1)
            divergence(i)
            combine(i)

        def drain_tile(i):
            drain(BANKS_PER_TILE)
            row_max(i)

        nc.scalar.dma_start(out=scale[:], in_=w_scale.rearrange("(g p t) o -> p g (t o)", p=P, t=PACK))
        for j in range(3):
            load_w(j)
        load_h(0)
        for j in range(3, len(pieces)):
            load_w(j)
        load_h(1)
        make_identity(nc, identity[:])
        nc.gpsimd.iota(ladder[:], pattern=[[1, STEPS]], base=0, channel_multiplier=0, allow_small_or_imprecise_dtypes=True)
        nc.scalar.activation(out=ladder[:], in_=ladder[:], func=ACT.Exp, scale=STEP, bias=-LOG_SPAN)
        turn(0)
        widen(0, on_vector=PACK // 2)
        widen(1, on_vector=PACK // 2)
        for j in range(len(pieces) - 2):
            if j >= 2:
                widen(j, on_vector=PACK // 2 if j == 2 else 0)
            if j == 2:
                regroup(0, nc.scalar.copy)
                turn(1)
            interleave(j, nc.vector.tensor_copy)
            if j > 0:
                quantize_w(j - 1)
            if j == 2:
                quantize_h(0)
            if j == 4:
                drain(2)
        widen(6)
        widen(7)
        drain(2)
        quantize_w(5)
        interleave(6, nc.scalar.copy)
        interleave(7, nc.vector.tensor_copy)
        regroup(1, nc.scalar.copy)
        turn(2)
        drain(2)
        quantize_w(7)
        quantize_w(6)
        regroup(2, nc.scalar.copy, d_slot=0)
        quantize_h(1)
        turn(3)
        drain(2)
        row_max(0)
        quantize_h(2)

        def drain_round(i):
            drain_tile(i + 1)
            guess(i)
            if i == 2:
                regroup(i + 3, nc.vector.tensor_copy, d_slot=i + 1)
            turn(i + 4)
            quantize_h(i + 3)
            subtract(i + 1, nc.gpsimd, d_slot=i + 1)

        subtract(0, nc.gpsimd, d_slot=0)
        exp(0)
        regroup(3, nc.scalar.copy, d_slot=1)
        drain_round(0)
        exp(1, then_shift=0)
        regroup(4, nc.scalar.copy, d_slot=2)
        drain_round(1)
        tanh(0, then_shift=1)
        exp(2)
        drain_round(2)
        tanh(1, then_shift=2)
        tanh(2)
        drain(CHUNKS)
        regroup(6, nc.vector.tensor_copy)
        drain(CHUNKS)
        turn(7)
        row_max(4)
        quantize_h(6)

        log(0)
        weigh(0, 0)
        weigh(0, 1)
        log(1)
        log(2)
        weigh(1, 0)
        divergence(0)
        weigh(1, 1)
        combine(0)
        divergence(1)
        regroup(7, nc.vector.tensor_copy, d_slot=0)
        combine(1)

        subtract(4, nc.gpsimd, d_slot=1)
        drain_tile(5)
        exp(3)
        exp(4)
        guess(3)
        guess(4)
        quantize_h(7)
        subtract(5, nc.gpsimd, d_slot=0)
        drain_tile(6)
        exp(5, then_shift=3)
        tanh(3, then_shift=4)
        guess(5)
        tanh(4, then_shift=5)
        tanh(5)
        finish(2)
        subtract(6, nc.gpsimd, d_slot=2)
        drain_tile(7)

        log(3)
        finish(3)
        log(4)
        log(5)
        weigh(4, 0)
        weigh(4, 1)

        exp(6)
        diff[7] = buffer("d3", [P, V], F32, "diff7")
        subtract_part(7, nc.vector, columns(0, 2))
        divergence(4)
        guess(6)
        subtract_part(7, nc.vector, columns(1, 2))
        combine(4)
        weigh(5, 0, 0, 2)
        exp(7, then_shift=6)
        guess(7)
        weigh(5, 0, 1, 2)
        weigh(5, 1, 0, 2)
        weigh(5, 1, 1, 2)
        tanh(6, then_shift=7)
        tanh(7)
        divergence(5)
        combine(5)

        log(6)
        log(7)
        for a in range(2):
            for half in range(2):
                weigh(6, a, half, 2)
        weigh(7, 0, 0, 2)
        divergence(6)
        weigh(7, 0, 1, 2)
        combine(6)
        weigh(7, 1, 0, 2)
        weigh(7, 1, 1, 2)
        divergence(7)
        combine(7, parts=4)
